import numpy as np, ml_dtypes
CORES = [2,6,10,14,18,22,26,30]
N = 8
BF = ml_dtypes.bfloat16
def gentries(a):
    return np.ascontiguousarray(a.reshape(8, 16, -1).transpose(0, 2, 1)).reshape(8, -1)
def gtable(e):
    e = np.asarray(e); return np.ascontiguousarray(e.reshape(8, -1, 16).transpose(0, 2, 1)).reshape(128, -1).astype(np.int32)
def f(rng, *shape):
    return (rng.standard_normal(shape, dtype=np.float32) * np.exp2(rng.integers(-2, 3, shape[:-1] + (1,)))).astype(BF)
def wide(rng, *shape):
    v = f(rng, *shape).astype(np.float32); k = shape[:-2] + (1, shape[-1])
    return (v * np.exp2(rng.integers(-6, 7, k)) * (rng.random(k) > 0.0625)).astype(BF)
R, G, NT, E, RD = 512, 192, 512, 4, 6
H, W = R // 2, R + N * G
def energies(rng, n):
    v = rng.standard_normal((N, 8, 16, n), dtype=np.float32) * np.exp2(rng.integers(-1, 2, (N, 8, 1, 1))).astype(np.float32)
    return v.reshape(N, 128, n).astype(BF)
def glist(e):
    return np.stack([gtable(v) for v in e])
def ungl(a):
    return np.stack([gentries(v) for v in a]).astype(np.int64)
def setup_inputs(rng):
    return {"own": energies(rng, R), "pair": energies(rng, 16 * NT), "st": rng.integers(0, 16, (N, 8, R)).astype(np.int32),
            "nb": glist(rng.integers(0, W, (N, 8, E * R))), "th": glist(rng.integers(0, W, (N, 8, E * R))), "tb": glist(rng.integers(0, NT, (N, 8, E * R))),
            "sd": glist(rng.integers(0, R, (N, 8, N * G)))}
def setup_inputs_ties(rng):
    d = setup_inputs(rng)
    own = rng.integers(0, 2, (N, 128, R)).astype(np.float32); pair = rng.integers(0, 3, (N, 128, 16 * NT)).astype(np.float32)
    q, g = int(rng.integers(0, N)), int(rng.integers(0, 8)); own[q, 16 * g:16 * g + 16] = 0; pair[q, 16 * g:16 * g + 16] = 0
    d["own"] = own.astype(BF); d["pair"] = pair.astype(BF); return d
def setup_inputs_ends(rng):
    d = setup_inputs(rng); v = np.array([0, H - 1, H, R - 1, R, R + G - 1, R + G, W - G, W - 1])
    d["nb"] = glist(rng.choice(v, (N, 8, E * R))); d["th"] = glist(rng.choice(v, (N, 8, E * R)))
    d["tb"] = glist(rng.choice(np.array([0, 1, NT - 2, NT - 1]), (N, 8, E * R))); d["sd"] = glist(rng.choice(np.array([0, H - 1, H, R - 1]), (N, 8, N * G)))
    d["st"] = rng.choice(np.array([0, 15]), (N, 8, R)).astype(np.int32)
    o = d["own"].astype(np.float32).reshape(N, 8, 16, R); o[:, :, 1:15] += 96; d["own"] = o.reshape(N, 128, R).astype(BF); return d
def setup_inputs_far(rng):
    d = setup_inputs(rng); q = (np.arange(N)[:, None, None] + 1 + np.arange(8)[None, :, None] % (N - 1)) % N
    m = np.tile(np.arange(E * R) % G, (N, 8, 1))
    d["nb"] = glist(R + G * q + rng.permuted(m, axis=2)); d["th"] = glist(R + G * q + rng.permuted(m, axis=2))
    d["sd"] = glist(rng.permuted(np.tile(np.arange(R), (N, 8, N, 1)), axis=3)[..., :G].reshape(N, 8, N * G))
    big = rng.random((N, 8, 1, 1)) < 0.5; b, g = int(rng.integers(0, N)), int(rng.integers(0, 8)); big[b, g] = True
    z = np.where(big, 2.0 ** 32, 1.0).astype(np.float32)
    o = d["own"].astype(np.float32).reshape(N, 8, 16, R); o[b, g] = np.abs(o[b, g]) + 64
    d["own"] = (o * z).reshape(N, 128, R).astype(BF)
    d["pair"] = (d["pair"].astype(np.float32).reshape(N, 8, 16, 16 * NT) * z).reshape(N, 128, 16 * NT).astype(BF); return d
def setup_inputs_alike(rng):
    d = setup_inputs(rng)
    for k, top in (("nb", W), ("th", W), ("tb", NT)):
        d[k] = glist(np.repeat(rng.integers(0, top, (N, 8, 2 * E)), H, axis=2))
    d["sd"] = glist(np.repeat(rng.integers(0, R, (N, 8, N)), G, axis=2))
    d["pair"] = (d["pair"].astype(np.float32) * np.float32(0.25)).astype(BF); return d
def setup_inputs_spread(rng):
    d = setup_inputs(rng); d["own"] = wide(rng, N, 128, R); d["pair"] = wide(rng, N, 128, 16 * NT); return d
def check_inputs(d):
    bad = []
    for k, top in (("nb", W), ("th", W), ("tb", NT), ("sd", R), ("st", 16)):
        if np.min(d[k]) < 0 or np.max(d[k]) >= top:
            bad.append(k)
    for k in ("own", "pair"):
        v = np.abs(d[k].astype(np.float32))
        if not np.all((v == 0) | ((v >= 2.0 ** -60) & (v <= 2.0 ** 40))):
            bad.append(k)
    return bad
def reference(own, pair, st, nb, th, tb, sd):
    a = own.astype(np.float32).reshape(N, 8, 16, R); p = pair.astype(np.float32).reshape(N, 8, 16, 16 * NT)
    s = st.astype(np.int64); low = np.zeros((N, 8, R), np.float32)
    near, third, base = [ungl(v).reshape(N, 8, 2, E * H) for v in (nb, th, tb)]; listed = ungl(sd)
    for t in range(RD):
        h = t & 1
        sent = np.take_along_axis(s, listed, 2).reshape(N, 8, N, G)
        w = np.concatenate([s, sent.transpose(2, 1, 0, 3).reshape(N, 8, N * G)], 2)
        col = 16 * ((base[:, :, h] + 37 * np.take_along_axis(w, third[:, :, h], 2)) & (NT - 1)) + np.take_along_axis(w, near[:, :, h], 2)
        x = np.take_along_axis(p, col[:, :, None, :], 3)
        v = a[:, :, :, h * H:(h + 1) * H]
        for k in range(E):
            v = v + x[:, :, :, k * H:(k + 1) * H]
        s[:, :, h * H:(h + 1) * H] = np.argmin(v, 2)
        low[:, :, h * H:(h + 1) * H] = np.min(v, 2)
    return {"y": s.astype(np.float32), "e": low}

@@ -1,0 +1,335 @@
+from concourse.bass import DstId, RemoteDMATransfer
+from concourse.mybir import AluOpType as Op, ActivationFunctionType as Act
+
+N, R, G, RD = 8, 512, 192, 6
+PAIR_CUTS = [0, 1536, 4608, 5632, 8192]
+NV = 12
+WIDE = 17088
+COPY_CUTS = [1536, 3776, 4864, 7104, 8192]
+
+BF, F32, I32, U16 = "bfloat16", "float32", "int32", "uint16"
+SCRATCH = {
+    "st32": ("sbuf", [128, 512], I32), "sd32": ("sbuf", [128, 96], I32), "sd16": ("sbuf", [128, 96], U16),
+    "l32": ("sbuf", [128, 256], I32), "l16": ("sbuf", [128, 256], U16), "cmp16": ("sbuf", [128, 256], U16),
+    "tb32": ("sbuf", [128, 128], I32), "tb16": ("sbuf", [128, 128], U16),
+    "ownb": ("sbuf", [128, 512], BF), "pairb": ("sbuf", [128, WIDE], BF),
+    "W": ("sbuf", [128, 4096], BF), "mapw": ("sbuf", [128, 2048], BF),
+    "sent": ("sbuf", [128, 1536], BF), "mrow": ("sbuf", [128, 1536], BF), "crow": ("sbuf", [128, 2048], BF),
+    "tbrow": ("sbuf", [128, 2048], BF), "ub": ("sbuf", [128, 1024], BF), "zb": ("sbuf", [128, 1024], BF),
+    "xb": ("sbuf", [128, 1024], BF),
+    "one": ("sbuf", [128, 144], BF), "neg": ("sbuf", [128, 144], BF), "onef": ("sbuf", [128, 128], F32),
+    "selA": ("sbuf", [128, 144], BF), "selB": ("sbuf", [128, 144], BF),
+    "idb": ("sbuf", [128, 128], BF), "idf": ("sbuf", [128, 128], F32),
+    "c0": ("sbuf", [128, 128], F32), "c2": ("sbuf", [128, 128], BF),
+    "qf": ("sbuf", [128, 256], F32), "qi": ("sbuf", [128, 256], I32), "qa": ("sbuf", [128, 256], F32),
+    "qn": ("sbuf", [128, 256], F32), "base": ("sbuf", [128, 256], F32),
+    "f1": ("sbuf", [128, 128], F32), "f2": ("sbuf", [128, 128], F32), "f3": ("sbuf", [128, 128], F32),
+    "o1": ("sbuf", [128, 64], I32), "o2": ("sbuf", [128, 64], I32), "off": ("sbuf", [128, 64], U16),
+    "rm0": ("sbuf", [128, 136], F32), "rm1": ("sbuf", [128, 136], F32),
+    "nf0": ("sbuf", [128, 128], BF), "nf1": ("sbuf", [128, 128], BF),
+    "s0": ("sbuf", [128, 128], BF), "s1": ("sbuf", [128, 128], BF),
+    "rows": ("sbuf", [128, 5 * 256], BF), "yrow": ("sbuf", [128, 512], F32), "erow": ("sbuf", [128, 512], F32),
+    "sendA": ("dram", [16, 128, 6], BF), "landA": ("dram", [64, 128, 6], BF),
+    "sendM": ("dram", [16, 128, 6], BF), "landM": ("dram", [64, 128, 6], BF),
+}
+for _t in range(RD):
+    SCRATCH["land%d" % _t] = ("dram", [64, 128, 2], BF)
+for _n in ("psO", "psV0", "psV1", "psB0", "psB1", "psE0", "psE1", "psC"):
+    SCRATCH[_n] = ("psum", [128, 512], F32)
+
+SEMAPHORES = (["v", "a", "p", "gq", "left", "iss", "arrA", "arrM"] + ["arr%d" % t for t in range(RD)]
+              + ["d%d" % i for i in range(40)])
+
+
+def rank_program(g, core, T, topo):
+    rank = T.rank_of(core)
+    if rank is None:
+        return
+    V, A, P, S = g.vector, g.scalar, g.tensor, g.sync
+    queue = {"v": V, "a": A, "p": P, "s": S, "gq": g}
+    count, seen, ndma = {}, {}, [0]
+
+    def wait(q, *marks):
+        for sem, val in marks:
+            if seen.get((q, sem), 0) < val:
+                queue[q].wait_ge(T.sem[sem], val)
+                seen[(q, sem)] = val
+
+    def done(q, ins):
+        count[q] = count.get(q, 0) + 1
+        ins.then_inc(T.sem[q], 1)
+        return (q, count[q])
+
+    def dma(q, out, in_):
+        sem = "d%d" % ndma[0]
+        ndma[0] += 1
+        queue[q].dma_start(out, in_).then_inc(T.sem[sem], 16)
+        count[sem] = 16
+        return (sem, 16)
+
+    peers = [r for r in range(N) if r != rank]
+    lanes = sorted(set.intersection(*[set(topo.engines(core, T.cores[r])) for r in peers]))
+
+    def dst_id(r):
+        rid, pid, _ = topo.addr(T.cores[r])
+        return DstId(rid=rid, pnc=pid)
+
+    def send(src_of, dst_of, ranks, sem):
+        tr = [RemoteDMATransfer(dst_ids=[dst_id(r) for r in ranks], dma_engine_mask=1 << lanes[k],
+                                remote_sem=T.sem[sem], srcs=[src_of(k)], dsts=[dst_of(k) for r in ranks])
+              for k in range(8)]
+        g.remote_dma_fused(tr, local_sem=T.sem.left)
+        count["left"] = count.get("left", 0) + 8
+        count[sem] = 8 * (N - 1)
+
+    W = T.W
+    row = slice(15, 128, 16)
+    mine = rank // 4
+
+    m_st = done("v", V.memset(T.st32[:], 0))
+    l_sd = dma("s", T.sd32[:], T.sd[:])
+    wait("a", m_st)
+    l_st = dma("a", T.st32[row, :], T.st[:])
+    l_tb = dma("s", T.tb32[:], T.tb[:])
+    l_nb = dma("s", T.l32[:, 0:128], T.nb[:])
+    l_th = dma("s", T.l32[:, 128:256], T.th[:])
+    l_own = dma("s", T.ownb[:], T.own[:])
+    l_pair = []
+
+    def load_pair():
+        a, b = PAIR_CUTS[len(l_pair)], PAIR_CUTS[len(l_pair) + 1]
+        l_pair.append(dma("s", T.pairb[:, a:b], T.pair[:, a:b]))
+
+    load_pair()
+    done("v", V.memset(T.one[:], 1.0))
+    done("v", V.memset(T.neg[:], -592.0))
+    m_one = done("v", V.memset(T.onef[:], 1.0))
+    m_c0 = done("v", V.memset(T.c0[:], 0.0))
+    done("v", V.memset(T.rm0[:, 0:8], 0.0))
+    done("v", V.memset(T.rm1[:, 0:8], 0.0))
+    wait("v", m_c0)
+    done("v", V.memset(T.c0[:, 0:128:16], 1e29))
+
+    g_iota = done("gq", g.iota(T.mapw[:, 0:512], [[1, 512]], -256, 0, allow_small_or_imprecise_dtypes=True))
+    done("gq", g.iota(T.c2[:], [[0, 8], [-1, 16]], 15, 0, allow_small_or_imprecise_dtypes=True))
+    wait("gq", m_one)
+    done("gq", g.affine_select(T.selA[:], T.one[:], [[-16, 9], [200, 16]], Op.is_equal, 0.0, -3015, 1))
+    done("gq", g.affine_select(T.selB[:], T.neg[:], [[-16, 9], [200, 16]], Op.is_equal, 0.0, -3015, 1))
+    done("gq", g.affine_select(T.idb[:], T.one[:, 0:128], [[-1, 128]], Op.is_equal, 0.0, 0, 1))
+    g_const = done("gq", g.affine_select(T.idf[:], T.onef[:], [[-1, 128]], Op.is_equal, 0.0, 0, 1))
+
+    def sel(m, r):
+        return m[:, 15 - r:143 - r]
+
+    wait("v", l_sd)
+    done("v", V.tensor_copy(T.sd16[:], T.sd32[:]))
+    wait("v", l_st)
+    c_st = done("v", V.tensor_scalar(W[:, 0:512], T.st32[:], -1.0, 15.0, Op.mult, Op.add))
+    wait("v", c_st)
+    wait("a", c_st)
+    sv = done("v", V.tensor_copy(T.sent[:, 0:768], W[:, 0:512].indirect(T.sd16[:, 0:48])))
+    sa = done("a", A.activation(T.sent[:, 768:1536], W[:, 0:512].indirect(T.sd16[:, 48:96]), Act.Copy))
+    wait("v", g_iota)
+    wait("a", g_iota)
+    mv = done("v", V.tensor_copy(T.mrow[:, 0:768], T.mapw[:, 0:512].indirect(T.sd16[:, 0:48])))
+    ma = done("a", A.activation(T.mrow[:, 768:1536], T.mapw[:, 0:512].indirect(T.sd16[:, 48:96]), Act.Copy))
+
+    wait("s", sv, sa)
+    outA = dma("s", T.sendA[:], T.sent[row, :])
+    ownA = dma("s", T.landA[rank:64:8], T.sent[row, 768 * mine:768 * mine + 768])
+    out0 = dma("s", T.land0[rank:64:8], W[row, 256:512])
+    wait("s", mv, ma)
+    outM = dma("s", T.sendM[:], T.mrow[row, :])
+    ownM = dma("s", T.landM[rank:64:8], T.mrow[row, 768 * mine:768 * mine + 768])
+    load_pair()
+
+    def send_halves(src, land, sem):
+        for hf in (1 - mine, mine):
+            send(lambda k: src[2 * k + hf], lambda k: land[8 * k + rank], [r for r in peers if r // 4 == hf], sem)
+
+    def send_states(t):
+        land = T["land%d" % t]
+        send(lambda k: land[8 * k + rank], lambda k: land[8 * k + rank], peers, "arr%d" % t)
+
+    wait("gq", outA)
+    send_halves(T.sendA, T.landA, "arrA")
+    g.sem_inc(T.sem.iss, 1)
+    count["iss"] = 1
+    wait("gq", out0)
+    send_states(0)
+    wait("gq", outM)
+    send_halves(T.sendM, T.landM, "arrM")
+
+    wait("v", l_tb)
+    c_tb = done("v", V.tensor_copy(T.tb16[:], T.tb32[:]))
+    m_w0 = done("v", V.memset(W[:, 512:2048], 0.0))
+    wait("v", l_nb, l_th)
+    c_l = done("v", V.tensor_copy(T.l16[:], T.l32[:]))
+    done("v", V.memset(T.mapw[:, 512:2048], 0.0))
+    m_w1 = done("v", V.memset(W[:, 2048:4096], 0.0))
+    x = done("v", V.tensor_scalar(T.qf[:], T.l32[:], -607.5, 1.0 / G, Op.add, Op.mult))
+    wait("v", x)
+    x = done("v", V.tensor_copy(T.qi[:], T.qf[:]))
+    wait("v", x)
+    done("v", V.tensor_scalar(T.qa[:], T.qi[:], -1.0, None, Op.max))
+    x = done("v", V.tensor_scalar(T.qn[:], T.qi[:], 0.0, float(rank + 1), Op.is_lt, Op.mult))
+    wait("v", x)
+    x = done("v", V.tensor_tensor(T.qf[:], T.qa[:], T.qn[:], Op.add))
+    wait("v", x)
+    c_base = done("v", V.tensor_scalar(T.base[:], T.qf[:], 256.0, 256.0, Op.mult, Op.add))
+    wait("v", l_pair[0])
+    done("v", V.tensor_copy(T.pairb[:, 8192:8192 + COPY_CUTS[0]], T.pairb[:, 0:COPY_CUTS[0]]))
+    done("v", V.tensor_copy(T.pairb[:, 16384:WIDE], T.pairb[:, 0:WIDE - 16384]))
+    wait("a", c_tb)
+    g_tb = [done("a", A.activation(T.tbrow[:, 1024 * h:1024 * h + 1024],
+                                   T.mapw[:, 0:512].indirect(T.tb16[:, 64 * h:64 * h + 64]), Act.Copy, scale=16.0))
+            for h in range(2)]
+
+    part = slice(32 * (rank % 4), 32 * (rank % 4) + 32)
+    wait("s", ("iss", 1))
+    load_pair()
+    wait("s", m_w0, ownA, ("arrA", 56))
+    window = dma("s", W[row, 512:2048], T.landA[:, part, :])
+    load_pair()
+    wait("s", m_w1, out0, ("arr0", 56))
+    in0 = dma("s", W[row, 2048:4096], T.land0[:])
+    wait("s", ownM, ("arrM", 56))
+    inM = dma("s", T.mapw[row, 512:2048], T.landM[:, part, :])
+
+    psV, psB, psE = [T.psV0, T.psV1], [T.psB0, T.psB1], [T.psE0, T.psE1]
+    rm, nf, sc = [T.rm0, T.rm1], [T.nf0, T.nf1], [T.s0, T.s1]
+
+    def open_round(t):
+        h = t & 1
+        wait("p", g_const, g_tb[h], l_own)
+        for r in range(16):
+            a = 1024 * h + 256 * (r % 4)
+            P.matmul(T.psO[:, 0:64], sel(T.selA, r), T.tbrow[:, a + r // 4:a + 256:4], r == 0, False)
+        for b in range(2):
+            a = 256 * h + 128 * b
+            P.matmul(psV[b][:, 0:128], T.ownb[:, a:a + 128], T.idb[:], True, False)
+
+    repeated = []
+
+    def compose(h):
+        wait("v", inM)
+        wait("a", inM)
+        cv = done("v", V.tensor_copy(T.crow[:, 0:1024], T.mapw[:, 0:2048].indirect(T.l16[:, 64 * h:64 * h + 64])))
+        ca = done("a", A.activation(T.crow[:, 1024:2048],
+                                    T.mapw[:, 0:2048].indirect(T.l16[:, 128 + 64 * h:192 + 64 * h]), Act.Copy))
+        a, b, c = COPY_CUTS[2 - 2 * h:5 - 2 * h]
+        done("v", V.tensor_copy(T.pairb[:, 8192 + a:8192 + b], T.pairb[:, a:b]))
+        repeated.append(done("a", A.activation(T.pairb[:, 8192 + b:8192 + c], T.pairb[:, b:c], Act.Copy)))
+        wait("p", cv, ca)
+        for r in range(16):
+            ins = P.matmul(T.psC[:, 0:128], sel(T.selA, r), T.crow[:, r:2048:16], r == 0, r == 15)
+        wait("v", done("p", ins), c_base)
+        x = done("v", V.tensor_scalar(T.f1[:], T.psC[:, 0:128], 0.0, 1792.0, Op.is_ge, Op.mult))
+        wait("v", x)
+        x = done("v", V.tensor_tensor(T.f2[:], T.psC[:, 0:128], T.f1[:], Op.add))
+        wait("v", x)
+        for j in range(2):
+            a = 128 * j + 64 * h
+            x = done("v", V.tensor_tensor(T.f3[:, 64 * j:64 * j + 64], T.f2[:, 64 * j:64 * j + 64],
+                                          T.base[:, a:a + 64], Op.add))
+        wait("v", x)
+        for j in range(2):
+            a = 128 * j + 64 * h
+            x = done("v", V.tensor_copy(T.cmp16[:, a:a + 64], T.f3[:, 64 * j:64 * j + 64]))
+        return x
+
+    open_round(0)
+    lists = c_l
+    for t in range(RD):
+        h, last = t & 1, t == RD - 1
+        win, tile = (W[:, 0:2048], T.l16) if t == 0 else (W[:, 0:4096], T.cmp16)
+        for q in ("v", "a"):
+            wait(q, lists, window)
+            if t == 1:
+                wait(q, in0)
+        for k in range(4):
+            a, c = 64 * h + 16 * k, 256 * k
+            u = done("v", V.tensor_scalar(T.ub[:, c:c + 256], win.indirect(tile[:, a:a + 16]), -1.0, None, Op.mult))
+            z = done("a", A.activation(T.zb[:, c:c + 256], win.indirect(tile[:, 128 + a:144 + a]), Act.Copy))
+            wait("p", u)
+            for j in range(4):
+                P.matmul(T.psO[:, 0:64], sel(T.selA, 4 * j + k), T.ub[:, c + j:c + 256:4], False, False)
+            wait("p", z)
+            for j in range(4):
+                ins = P.matmul(T.psO[:, 0:64], sel(T.selB, 4 * j + k), T.zb[:, c + j:c + 256:4], False,
+                               k == 3 and j == 3)
+        wait("v", done("p", ins))
+        if t < 2:
+            x = done("v", V.tensor_scalar(T.o1[:], T.psO[:, 0:64], 12991.0, None, Op.add))
+            wait("v", x)
+            x = done("v", V.tensor_scalar(T.o2[:], T.o1[:], 8191, None, Op.bitwise_and))
+            wait("v", x)
+            x = done("v", V.tensor_copy(T.off[:], T.o2[:]))
+            tables = T.pairb[:, 0:8192]
+        else:
+            x = done("v", V.tensor_scalar(T.off[:], T.psO[:, 0:64], 12991.0, None, Op.add))
+            tables = T.pairb[:, 0:WIDE]
+        wait("v", x, *l_pair, *repeated)
+        wait("a", x, *l_pair, *repeated)
+        summed = []
+        for b, (c0, c1, c2) in enumerate(((0, 16, 32), (32, 32 + NV, 64))):
+            xv = done("v", V.tensor_copy(T.xb[:, 16 * c0:16 * c1], tables.indirect(T.off[:, c0:c1])))
+            xa = done("a", A.activation(T.xb[:, 16 * c1:16 * c2], tables.indirect(T.off[:, c1:c2]), Act.Copy))
+            wait("p", xv, xa)
+            for k in range(4):
+                ins = P.matmul(psV[b][:, 0:128], T.xb[:, 512 * b + k:512 * b + 512:4], T.idb[:], False, k == 3)
+            summed.append(done("p", ins))
+        back, low = [], []
+        for b in range(2):
+            wait("v", summed[b], g_const)
+            s1 = done("v", V.tensor_tensor_scan(rm[b][:, 1:129], T.c0[:], psV[b][:, 0:128], 0.0, Op.add, Op.min))
+            wait("v", s1)
+            x = done("v", V.tensor_tensor(nf[b][:], psV[b][:, 0:128], rm[b][:, 0:128], Op.is_ge))
+            wait("v", x)
+            s2 = done("v", V.tensor_tensor_scan(sc[b][:], nf[b][:], T.c2[:], 0.0, Op.mult, Op.max))
+            if last:
+                wait("p", s1)
+                low.append(done("p", P.transpose(psE[b][0:8, 0:128], rm[b][:, 16:129:16], T.idf[:])))
+            wait("p", s2)
+            back.append(done("p", P.matmul(psB[b][0:8, 0:128], sc[b][:, 15:128:16], T.idb[:], True, True)))
+        if not last:
+            c = 256 * t
+            wait("a", back[0])
+            r0 = done("a", A.activation(T.rows[0:8, c:c + 128], T.psB0[0:8, 0:128], Act.Copy))
+            wait("v", back[1])
+            r1 = done("v", V.tensor_copy(T.rows[0:8, c + 128:c + 256], T.psB1[0:8, 0:128]))
+            land = T["land%d" % (t + 1)]
+            wait("s", r0, r1)
+            out = dma("s", land[rank:64:8], T.rows[0:8, c:c + 256])
+            wait("gq", out)
+            send_states(t + 1)
+            wait("s", out, ("arr%d" % (t + 1), 56))
+            window = dma("s", W[row, 2048 * h:2048 * h + 2048], land[:])
+            if t == RD - 2:
+                for b in range(2):
+                    low.append(done("p", P.transpose(psE[b][0:8, 0:128], rm[b][:, 16:129:16], T.idf[:])))
+                    wait("a", low[b])
+                    x = done("a", A.activation(T.erow[0:8, 128 * b:128 * b + 128], psE[b][0:8, 0:128], Act.Copy))
+                wait("p", x)
+                wait("v", r0, r1)
+                done("v", V.tensor_scalar(T.yrow[0:8, 0:256], T.rows[0:8, c:c + 256], -1.0, 15.0, Op.mult, Op.add))
+            open_round(t + 1)
+            if t < 2:
+                lists = compose(1 - t)
+        else:
+            wait("a", low[0])
+            done("a", A.activation(T.erow[0:8, 256:384], T.psE0[0:8, 0:128], Act.Copy))
+            wait("a", back[0])
+            y0 = done("a", A.activation(T.yrow[0:8, 256:384], T.psB0[0:8, 0:128], Act.Identity, bias=15.0, scale=-1.0))
+            wait("a", low[1])
+            e1 = done("a", A.activation(T.erow[0:8, 384:512], T.psE1[0:8, 0:128], Act.Copy))
+            wait("v", back[1])
+            y1 = done("v", V.tensor_scalar(T.yrow[0:8, 384:512], T.psB1[0:8, 0:128], -1.0, 15.0, Op.mult, Op.add))
+            wait("a", e1)
+            wait("a", dma("a", T.e[:], T.erow[0:8, :]))
+            wait("s", y0, y1)
+            wait("s", dma("s", T.y[:], T.yrow[0:8, :]))
+
+    for sem, val in count.items():
+        if max([v for (q, s), v in seen.items() if s == sem] + [0]) < val:
+            wait("gq", (sem, val))

@@ -2,52 +2,70 @@ from concourse.bass import DstId, RemoteDMATransfer
 from concourse.mybir import AluOpType as Op, ActivationFunctionType as Act
 
 N, R, G, RD = 8, 512, 192, 6
-PAIR_CUTS = [0, 1536, 4608, 5632, 8192]
-NV = 12
+CUTS = [0, 1536, 3584, 5632, 7168, 8192]
+NCH = len(CUTS) - 1
+LONG = 3
 WIDE = 17088
-COPY_CUTS = [1536, 3776, 4864, 7104, 8192]
 
 BF, F32, I32, U16 = "bfloat16", "float32", "int32", "uint16"
 SCRATCH = {
-    "st32": ("sbuf", [128, 512], I32), "sd32": ("sbuf", [128, 96], I32), "sd16": ("sbuf", [128, 96], U16),
+    "XS": ("dram", [64, 128, 64], I32),
+    "XO": ("dram", [64, 128, 8], F32),
     "l32": ("sbuf", [128, 256], I32), "l16": ("sbuf", [128, 256], U16), "cmp16": ("sbuf", [128, 256], U16),
-    "tb32": ("sbuf", [128, 128], I32), "tb16": ("sbuf", [128, 128], U16),
-    "ownb": ("sbuf", [128, 512], BF), "pairb": ("sbuf", [128, WIDE], BF),
-    "W": ("sbuf", [128, 4096], BF), "mapw": ("sbuf", [128, 2048], BF),
-    "sent": ("sbuf", [128, 1536], BF), "mrow": ("sbuf", [128, 1536], BF), "crow": ("sbuf", [128, 2048], BF),
-    "tbrow": ("sbuf", [128, 2048], BF), "ub": ("sbuf", [128, 1024], BF), "zb": ("sbuf", [128, 1024], BF),
-    "xb": ("sbuf", [128, 1024], BF),
-    "one": ("sbuf", [128, 144], BF), "neg": ("sbuf", [128, 144], BF), "onef": ("sbuf", [128, 128], F32),
-    "selA": ("sbuf", [128, 144], BF), "selB": ("sbuf", [128, 144], BF),
-    "idb": ("sbuf", [128, 128], BF), "idf": ("sbuf", [128, 128], F32),
+    "tb32": ("sbuf", [128, 128], I32), "tbb": ("sbuf", [128, 128], BF), "tbw": ("sbuf", [128, 128], BF),
+    "sd32": ("sbuf", [128, 96], I32), "rot": ("sbuf", [128, 96], BF), "sdr": ("sbuf", [128, 96], F32),
+    "sd16": ("sbuf", [128, 96], U16), "st32": ("sbuf", [128, 32], I32), "stp": ("sbuf", [128, 224], BF),
+    "tab": ("sbuf", [128, R + WIDE], BF),
+    "W": ("sbuf", [128, 4096], BF), "mapw": ("sbuf", [128, 2048], BF), "crow": ("sbuf", [128, 4096], BF),
+    "ub": ("sbuf", [128, 1024], BF), "zb": ("sbuf", [128, 1024], BF), "xb": ("sbuf", [128, 1024], BF),
+    "nI": ("sbuf", [128, 256], BF), "p8": ("sbuf", [128, 8], I32), "e8": ("sbuf", [128, 8], I32),
+    "iv": ("sbuf", [128, 8], I32), "fv": ("sbuf", [128, 8], F32), "col": ("sbuf", [128, 16], F32),
+    "bq": ("sbuf", [128, 8], F32), "bx": ("sbuf", [128, 8], F32),
+    "t1": ("sbuf", [128, 16], F32), "t2": ("sbuf", [128, 16], F32), "t3": ("sbuf", [128, 16], F32),
+    "rotL": ("sbuf", [128, 16], U16), "repL": ("sbuf", [128, 8], U16),
+    "Z": ("sbuf", [128, 2048], BF), "R2": ("sbuf", [128, 256], BF), "idf": ("sbuf", [128, 128], F32),
+    "selU": ("sbuf", [128, 8], BF), "selZ": ("sbuf", [128, 8], BF), "selC": ("sbuf", [128, 8], BF),
     "c0": ("sbuf", [128, 128], F32), "c2": ("sbuf", [128, 128], BF),
-    "qf": ("sbuf", [128, 256], F32), "qi": ("sbuf", [128, 256], I32), "qa": ("sbuf", [128, 256], F32),
-    "qn": ("sbuf", [128, 256], F32), "base": ("sbuf", [128, 256], F32),
-    "f1": ("sbuf", [128, 128], F32), "f2": ("sbuf", [128, 128], F32), "f3": ("sbuf", [128, 128], F32),
     "o1": ("sbuf", [128, 64], I32), "o2": ("sbuf", [128, 64], I32), "off": ("sbuf", [128, 64], U16),
-    "rm0": ("sbuf", [128, 136], F32), "rm1": ("sbuf", [128, 136], F32),
     "nf0": ("sbuf", [128, 128], BF), "nf1": ("sbuf", [128, 128], BF),
-    "s0": ("sbuf", [128, 128], BF), "s1": ("sbuf", [128, 128], BF),
-    "rows": ("sbuf", [128, 5 * 256], BF), "yrow": ("sbuf", [128, 512], F32), "erow": ("sbuf", [128, 512], F32),
-    "sendA": ("dram", [16, 128, 6], BF), "landA": ("dram", [64, 128, 6], BF),
-    "sendM": ("dram", [16, 128, 6], BF), "landM": ("dram", [64, 128, 6], BF),
+    "rep0": ("sbuf", [128, 144], BF), "rep1": ("sbuf", [128, 144], BF), "repI": ("sbuf", [128, 528], BF),
+    "res": ("sbuf", [128, 1024], F32),
 }
-for _t in range(RD):
-    SCRATCH["land%d" % _t] = ("dram", [64, 128, 2], BF)
-for _n in ("psO", "psV0", "psV1", "psB0", "psB1", "psE0", "psE1", "psC"):
+for _x in range(4):
+    SCRATCH["rm%d" % _x] = ("sbuf", [128, 136], F32)
+    SCRATCH["s%d" % _x] = ("sbuf", [128, 128], BF)
+    SCRATCH["psT%d" % _x] = ("psum", [128, 1024], BF)
+for _c in range(NCH):
+    _w = CUTS[_c + 1] - CUTS[_c] + (R if _c == 0 else 0)
+    SCRATCH["stage%d" % _c] = ("dram", [8, 128, _w // 8], BF)
+    SCRATCH["land%d" % _c] = ("dram", [8, 128, _w // 8], BF)
+for _n in ("psO0", "psO1", "psV0", "psV1"):
     SCRATCH[_n] = ("psum", [128, 512], F32)
 
-SEMAPHORES = (["v", "a", "p", "gq", "left", "iss", "arrA", "arrM"] + ["arr%d" % t for t in range(RD)]
-              + ["d%d" % i for i in range(40)])
+SEMAPHORES = (["v", "a", "p", "gq", "left", "iss", "arrS", "arrO", "again"] + ["arr%d" % c for c in range(NCH)]
+              + ["rel%d" % c for c in range(LONG)] + ["fin%d" % c for c in range(LONG)]
+              + ["d%d" % i for i in range(60)])
 
 
 def rank_program(g, core, T, topo):
     rank = T.rank_of(core)
-    if rank is None:
+
+    def helpers(r):
+        me = T.cores[r]
+        near = [k for k in topo.cores_of(me) if topo.die(k) == topo.die(me) and k not in T.cores]
+        free = [k for k in near if all(topo.may_write(k, c) for c in T.cores)][0]
+        rest = [k for k in near if k != free]
+        return {"any": free, "plane": rest[0], "gather": rest[1]}
+
+    role = [(r, name) for r in range(N) for name, k in helpers(r).items() if k == core]
+    if rank is None and not role:
         return
-    V, A, P, S = g.vector, g.scalar, g.tensor, g.sync
-    queue = {"v": V, "a": A, "p": P, "s": S, "gq": g}
+    queue = {"s": g.sync, "gq": g}
+    if rank is not None:
+        V, A, P = g.vector, g.scalar, g.tensor
+        queue.update({"v": V, "a": A, "p": P})
     count, seen, ndma = {}, {}, [0]
+    tab = T.tab
 
     def wait(q, *marks):
         for sem, val in marks:
@@ -60,276 +78,409 @@ def rank_program(g, core, T, topo):
         ins.then_inc(T.sem[q], 1)
         return (q, count[q])
 
-    def dma(q, out, in_):
+    def dma(q, *copies):
         sem = "d%d" % ndma[0]
         ndma[0] += 1
-        queue[q].dma_start(out, in_).then_inc(T.sem[sem], 16)
-        count[sem] = 16
-        return (sem, 16)
+        for out, in_ in copies:
+            queue[q].dma_start(out, in_).then_inc(T.sem[sem], 16)
+        count[sem] = 16 * len(copies)
+        return (sem, count[sem])
 
-    peers = [r for r in range(N) if r != rank]
-    lanes = sorted(set.intersection(*[set(topo.engines(core, T.cores[r])) for r in peers]))
+    def engine_plan(src, turn, near):
+        me = T.cores[src]
+        order = [(src + 1 + i) % N for i in range(N - 1)]
+        far = [r for r in order if topo.chip(T.cores[r]) != topo.chip(me)]
+        lanes = sorted(set.intersection(*[set(topo.engines(me, T.cores[r])) for r in far]))
+        one, two = lanes[turn % 2::2], lanes[1 - turn % 2::2]
+        sets = [[e] for e in one] + [two[0:2], two[2:4]]
+        plan = {far[(i + 2 * turn) % len(far)]: sets[i] for i in range(len(far))}
+        for r in order:
+            if r not in plan:
+                plan[r] = [e for e in topo.engines(me, T.cores[r]) if e not in lanes][:near]
+        return plan
 
-    def dst_id(r):
-        rid, pid, _ = topo.addr(T.cores[r])
-        return DstId(rid=rid, pnc=pid)
+    def send(src_of, dst_of, sem, turn, near):
+        fused([(src_of(r), T.cores[r], dst_of(r), sem, engines) for r, engines in engine_plan(rank, turn, near).items()])
+        count[sem] = sum(len(engine_plan(q, turn, near)[rank]) for q in range(N) if q != rank)
+        return (sem, count[sem])
 
-    def send(src_of, dst_of, ranks, sem):
-        tr = [RemoteDMATransfer(dst_ids=[dst_id(r) for r in ranks], dma_engine_mask=1 << lanes[k],
-                                remote_sem=T.sem[sem], srcs=[src_of(k)], dsts=[dst_of(k) for r in ranks])
-              for k in range(8)]
+    def fused(writes):
+        tr = []
+        for src, to, dst, sem, engines in writes:
+            rid, pid, _ = topo.addr(to)
+            tr.append(RemoteDMATransfer(dst_ids=[DstId(rid=rid, pnc=pid)], dma_engine_mask=sum(1 << e for e in engines),
+                                        remote_sem=T.sem[sem], srcs=[src], dsts=[dst]))
         g.remote_dma_fused(tr, local_sem=T.sem.left)
-        count["left"] = count.get("left", 0) + 8
-        count[sem] = 8 * (N - 1)
+        count["left"] = count.get("left", 0) + sum(len(w[4]) for w in writes)
 
-    W = T.W
-    row = slice(15, 128, 16)
-    mine = rank // 4
+    def long_plan(src):
+        me, hs = T.cores[src], helpers(src)
+        order = [(src + 1 + i) % N for i in range(N - 1)]
+        far = [r for r in order if topo.chip(T.cores[r]) != topo.chip(me)]
+        plane = [r for r in far if topo.may_write(hs["plane"], T.cores[r])]
+        cross = [r for r in far if r not in plane]
+        lanes = topo.engines(me, T.cores[far[0]])
+        spare = [e for e in topo.engines(me, hs["any"]) if e not in lanes]
+        ways = ([(r, None) for r in cross[:2]] + [(r, hs["any"]) for r in cross[2:]]
+                + [(r, None) for r in order if r not in far] + [(src, None)] + [(r, hs["plane"]) for r in plane])
+        sets = [lanes[0:4:2], lanes[4:8:2], lanes[1:4:2], lanes[5:8:2], spare[0:4:2], spare[1:4:2], spare[4:6], spare[6:8]]
+        return {r: (via, engines) for (r, via), engines in zip(ways, sets)}
 
-    m_st = done("v", V.memset(T.st32[:], 0))
-    l_sd = dma("s", T.sd32[:], T.sd[:])
-    wait("a", m_st)
-    l_st = dma("a", T.st32[row, :], T.st[:])
-    l_tb = dma("s", T.tb32[:], T.tb[:])
-    l_nb = dma("s", T.l32[:, 0:128], T.nb[:])
-    l_th = dma("s", T.l32[:, 128:256], T.th[:])
-    l_own = dma("s", T.ownb[:], T.own[:])
-    l_pair = []
+    def cut(c):
+        buf = T["land%d" % c]
+        return CUTS[c], CUTS[c + 1], 16 * (CUTS[c + 1] - CUTS[c]) // buf.shape[2]
 
-    def load_pair():
-        a, b = PAIR_CUTS[len(l_pair)], PAIR_CUTS[len(l_pair) + 1]
-        l_pair.append(dma("s", T.pairb[:, a:b], T.pair[:, a:b]))
+    def lay_out(c, runs):
+        a, b, rows = cut(c)
+        buf = T["land%d" % c]
+        return ([(tab[16 * x:16 * y, R + a:R + b], buf[x:y, 0:rows, :]) for x, y in runs]
+                + [(tab[16 * x:16 * y, 0:R], buf[x:y, rows:128, :]) for x, y in runs if c == 0])
 
-    load_pair()
-    done("v", V.memset(T.one[:], 1.0))
-    done("v", V.memset(T.neg[:], -592.0))
-    m_one = done("v", V.memset(T.onef[:], 1.0))
-    m_c0 = done("v", V.memset(T.c0[:], 0.0))
-    done("v", V.memset(T.rm0[:, 0:8], 0.0))
-    done("v", V.memset(T.rm1[:, 0:8], 0.0))
-    wait("v", m_c0)
+    def finish():
+        for sem, val in count.items():
+            if max([v for (q, s), v in seen.items() if s == sem] + [0]) < val:
+                wait("gq", (sem, val))
+
+    if rank is None:
+        owner, name = role[0]
+        to = T.cores[owner]
+        for c in range(LONG):
+            if name == "gather":
+                wait("s", ("arr%d" % c, sum(2 if long_plan(q)[owner][0] is None else 4 for q in range(N))))
+                wait("gq", dma("s", *lay_out(c, [(0, N)])))
+                cols = slice(0 if c == 0 else R + CUTS[c], R + CUTS[c + 1])
+                fused([(tab[:, cols], to, tab[:, cols], "fin%d" % c, topo.engines(core, to))])
+            else:
+                mine = [r for r, (via, engines) in long_plan(owner).items() if via == core]
+                wait("gq", ("rel%d" % c, 2 * len(mine)))
+                lanes = topo.engines(core, T.cores[mine[0]])
+                fused([(T["stage%d" % c][r], helpers(r)["gather"], T["land%d" % c][owner], "arr%d" % c,
+                        lanes[4 * i:4 * i + 4]) for i, r in enumerate(mine)])
+        if name == "gather":
+            for a, n in ((8192, CUTS[LONG]), (16384, WIDE - 16384)):
+                fused([(tab[:, R:R + n], to, tab[:, R + a:R + a + n], "again", topo.engines(core, to))])
+        finish()
+        return
+
+    W, XS, col, nI = T.W, T.XS, T.col, T.nI
+    ident = T.Z[:, 0:128]
+    others = [(a, b) for a, b in ((0, rank), (rank + 1, N)) if a < b]
+    mine = slice(16 * rank, 16 * rank + 16)
+    outs, ins_ = slice(rank, 64, 8), slice(8 * rank, 8 * rank + 8)
+    all_engines = len(topo.engines(helpers(rank)["gather"], core))
+    psO, psV, psT = [T.psO0, T.psO1], [T.psV0, T.psV1], [T["psT%d" % x] for x in range(4)]
+    rm, sc = [T["rm%d" % x] for x in range(4)], [T["s%d" % x] for x in range(4)]
+    nf, rep = [T.nf0, T.nf1], [T.rep0, T.rep1]
+
+    def stage(c):
+        a, b, rows = cut(c)
+        buf, runs = T["stage%d" % c], [(0, N)] if c < LONG else others
+        return dma("s", *([(buf[x:y, 0:rows, :], T.pair[16 * x:16 * y, a:b]) for x, y in runs]
+                          + [(buf[x:y, rows:128, :], T.own[16 * x:16 * y, :]) for x, y in runs if c == 0]))
+
+    sS = [dma("s", (XS[outs, 0:32, :], T.nb[:]), (XS[outs, 32:64, :], T.th[:]), (XS[outs, 64:96, :], T.tb[:])),
+          dma("a", (XS[outs, 96:120, :], T.sd[:]), (XS[outs, 120:128, :], T.st[:]))]
+    staged = [stage(0)]
+
+    g_p = done("gq", g.iota(T.p8[:], [[0, 8]], 0, 1))
+    g_n = done("gq", g.iota(nI[:], [[0, 2], [1, 128]], 0, 0, allow_small_or_imprecise_dtypes=True))
+    g_c2 = done("gq", g.iota(T.c2[:], [[0, 8], [-1, 16]], 15, 0, allow_small_or_imprecise_dtypes=True))
+
+    def ts(out, in0, s1, s2, op0, op1=None):
+        if op1 is None:
+            return done("v", V.tensor_scalar(out, in0, s1, None, op0))
+        return done("v", V.tensor_scalar(out, in0, s1, s2, op0, op1))
+
+    x = done("v", V.memset(T.c0[:], 0.0))
+    for buf in [T.stp[:], T.rep0[:, 128:144], T.rep1[:, 128:144], T.repI[:, 512:528]] + [m[:, 0:8] for m in rm]:
+        done("v", V.memset(buf, 0.0))
+    wait("v", x, g_p)
     done("v", V.memset(T.c0[:, 0:128:16], 1e29))
+    p1 = T.p8[:, 0:1]
+    ts(T.iv[:, 0:1], p1, 127, None, Op.bitwise_and)
+    ts(T.iv[:, 1:2], p1, 4, None, Op.arith_shift_right)
+    ts(T.iv[:, 2:3], p1, 15, None, Op.bitwise_and)
+    x = ts(T.e8[:], T.p8[:], 7, None, Op.bitwise_and)
+    wait("v", x)
+    x = done("v", V.tensor_copy(T.fv[:, 0:3], T.iv[:, 0:3]))
+    ts(T.repL[:], T.e8[:], 16.0, 15.0, Op.mult, Op.add)
+    wait("v", x, g_n)
+    pf, gf, lf = [T.fv[:, i:i + 1] for i in range(3)]
+    cM0, cM1, cU, cZ, cH, cR, cD, cE, cC = [col[:, i:i + 1] for i in range(9)]
+    c_z = ts(T.Z[:, 0:256], nI[:], pf, None, Op.is_equal)
+    ts(cD, gf, -12.0, lf, Op.mult, Op.add)
+    ts(cE, gf, 12.0, lf, Op.mult, Op.add)
+    ts(cR, gf, -16.0, lf, Op.mult, Op.add)
+    ts(cM0, lf, 0.0, None, Op.is_equal)
+    ts(cM1, lf, 1.0, None, Op.is_equal)
+    ts(cU, lf, 0.0, -1.0, Op.is_equal, Op.mult)
+    ts(cZ, lf, 0.0, -592.0, Op.is_equal, Op.mult)
+    ts(cH, lf, 1.0, 128.0, Op.is_equal, Op.mult)
+    x = ts(T.t3[:, 12:16], nI[:, 0:4], 8.0, gf, Op.mult, Op.add)
+    wait("v", x)
+    ts(T.t1[:, 0:6], nI[:, 0:6], 16.0, cD, Op.mult, Op.add)
+    ts(T.t1[:, 6:12], nI[:, 0:6], 16.0, cE, Op.mult, Op.add)
+    ts(cC, cM0, cH, None, Op.add)
+    ts(T.bq[:], nI[:, 0:8], gf, cM1, Op.subtract, Op.mult)
+    x = ts(T.bx[:, 0:4], T.t3[:, 12:16], cM1, None, Op.mult)
+    ts(T.R2[:], nI[:], -112.0, cR, Op.add, Op.is_equal)
+    wait("v", x)
+    ts(T.t2[:, 0:6], T.t1[:, 0:6], 0.0, 96.0, Op.is_lt, Op.mult)
+    x = ts(T.t2[:, 6:12], T.t1[:, 6:12], 96.0, -96.0, Op.is_ge, Op.mult)
+    for m, w in ((T.selC, cC), (T.selU, cU), (T.selZ, cZ)):
+        ts(m[:], nI[:, 0:8], gf, w, Op.is_equal, Op.mult)
+    wait("v", x)
+    x = done("v", V.tensor_tensor(T.t3[:, 0:12], T.t1[:, 0:12], T.t2[:, 0:12], Op.add))
+    for a in range(4):
+        ts(T.mapw[:, 128 * a:128 * a + 128], nI[:, 0:128], cM0, T.bx[:, a:a + 1], Op.mult, Op.add)
+    wait("v", x)
+    c_const = done("v", V.tensor_copy(T.rotL[:, 0:12], T.t3[:, 0:12]))
+    x = c_z
+    for n in (256, 512, 1024):
+        wait("a", x)
+        x = done("a", A.activation(T.Z[:, n:2 * n], T.Z[:, 0:n], Act.Copy))
+    c_Z = x
+    done("a", A.activation(T.idf[:], ident, Act.Copy))
 
-    g_iota = done("gq", g.iota(T.mapw[:, 0:512], [[1, 512]], -256, 0, allow_small_or_imprecise_dtypes=True))
-    done("gq", g.iota(T.c2[:], [[0, 8], [-1, 16]], 15, 0, allow_small_or_imprecise_dtypes=True))
-    wait("gq", m_one)
-    done("gq", g.affine_select(T.selA[:], T.one[:], [[-16, 9], [200, 16]], Op.is_equal, 0.0, -3015, 1))
-    done("gq", g.affine_select(T.selB[:], T.neg[:], [[-16, 9], [200, 16]], Op.is_equal, 0.0, -3015, 1))
-    done("gq", g.affine_select(T.idb[:], T.one[:, 0:128], [[-1, 128]], Op.is_equal, 0.0, 0, 1))
-    g_const = done("gq", g.affine_select(T.idf[:], T.onef[:], [[-1, 128]], Op.is_equal, 0.0, 0, 1))
+    arrived = {}
 
-    def sel(m, r):
-        return m[:, 15 - r:143 - r]
+    def send_chunk(c):
+        wait("gq", staged[c])
+        st_, la = T["stage%d" % c], T["land%d" % c]
+        if c >= LONG:
+            arrived[c] = send(lambda r: st_[r], lambda r: la[rank], "arr%d" % c, c + 1, 8)
+            return
+        fused([(st_[r], via, st_[r], "rel%d" % c, engines) if via is not None
+               else (st_[r], helpers(r)["gather"], la[rank], "arr%d" % c, engines)
+               for r, (via, engines) in long_plan(rank).items()])
+        count["fin%d" % c] = all_engines
 
-    wait("v", l_sd)
-    done("v", V.tensor_copy(T.sd16[:], T.sd32[:]))
-    wait("v", l_st)
-    c_st = done("v", V.tensor_scalar(W[:, 0:512], T.st32[:], -1.0, 15.0, Op.mult, Op.add))
-    wait("v", c_st)
-    wait("a", c_st)
-    sv = done("v", V.tensor_copy(T.sent[:, 0:768], W[:, 0:512].indirect(T.sd16[:, 0:48])))
-    sa = done("a", A.activation(T.sent[:, 768:1536], W[:, 0:512].indirect(T.sd16[:, 48:96]), Act.Copy))
-    wait("v", g_iota)
-    wait("a", g_iota)
-    mv = done("v", V.tensor_copy(T.mrow[:, 0:768], T.mapw[:, 0:512].indirect(T.sd16[:, 0:48])))
-    ma = done("a", A.activation(T.mrow[:, 768:1536], T.mapw[:, 0:512].indirect(T.sd16[:, 48:96]), Act.Copy))
-
-    wait("s", sv, sa)
-    outA = dma("s", T.sendA[:], T.sent[row, :])
-    ownA = dma("s", T.landA[rank:64:8], T.sent[row, 768 * mine:768 * mine + 768])
-    out0 = dma("s", T.land0[rank:64:8], W[row, 256:512])
-    wait("s", mv, ma)
-    outM = dma("s", T.sendM[:], T.mrow[row, :])
-    ownM = dma("s", T.landM[rank:64:8], T.mrow[row, 768 * mine:768 * mine + 768])
-    load_pair()
-
-    def send_halves(src, land, sem):
-        for hf in (1 - mine, mine):
-            send(lambda k: src[2 * k + hf], lambda k: land[8 * k + rank], [r for r in peers if r // 4 == hf], sem)
-
-    def send_states(t):
-        land = T["land%d" % t]
-        send(lambda k: land[8 * k + rank], lambda k: land[8 * k + rank], peers, "arr%d" % t)
-
-    wait("gq", outA)
-    send_halves(T.sendA, T.landA, "arrA")
+    wait("gq", *sS)
+    arrS = send(lambda r: XS[8 * r + rank], lambda r: XS[8 * r + rank], "arrS", 0, 2)
     g.sem_inc(T.sem.iss, 1)
     count["iss"] = 1
-    wait("gq", out0)
-    send_states(0)
-    wait("gq", outM)
-    send_halves(T.sendM, T.landM, "arrM")
-
-    wait("v", l_tb)
-    c_tb = done("v", V.tensor_copy(T.tb16[:], T.tb32[:]))
-    m_w0 = done("v", V.memset(W[:, 512:2048], 0.0))
-    wait("v", l_nb, l_th)
-    c_l = done("v", V.tensor_copy(T.l16[:], T.l32[:]))
-    done("v", V.memset(T.mapw[:, 512:2048], 0.0))
-    m_w1 = done("v", V.memset(W[:, 2048:4096], 0.0))
-    x = done("v", V.tensor_scalar(T.qf[:], T.l32[:], -607.5, 1.0 / G, Op.add, Op.mult))
-    wait("v", x)
-    x = done("v", V.tensor_copy(T.qi[:], T.qf[:]))
-    wait("v", x)
-    done("v", V.tensor_scalar(T.qa[:], T.qi[:], -1.0, None, Op.max))
-    x = done("v", V.tensor_scalar(T.qn[:], T.qi[:], 0.0, float(rank + 1), Op.is_lt, Op.mult))
-    wait("v", x)
-    x = done("v", V.tensor_tensor(T.qf[:], T.qa[:], T.qn[:], Op.add))
-    wait("v", x)
-    c_base = done("v", V.tensor_scalar(T.base[:], T.qf[:], 256.0, 256.0, Op.mult, Op.add))
-    wait("v", l_pair[0])
-    done("v", V.tensor_copy(T.pairb[:, 8192:8192 + COPY_CUTS[0]], T.pairb[:, 0:COPY_CUTS[0]]))
-    done("v", V.tensor_copy(T.pairb[:, 16384:WIDE], T.pairb[:, 0:WIDE - 16384]))
-    wait("a", c_tb)
-    g_tb = [done("a", A.activation(T.tbrow[:, 1024 * h:1024 * h + 1024],
-                                   T.mapw[:, 0:512].indirect(T.tb16[:, 64 * h:64 * h + 64]), Act.Copy, scale=16.0))
-            for h in range(2)]
-
-    part = slice(32 * (rank % 4), 32 * (rank % 4) + 32)
+    send_chunk(0)
     wait("s", ("iss", 1))
-    load_pair()
-    wait("s", m_w0, ownA, ("arrA", 56))
-    window = dma("s", W[row, 512:2048], T.landA[:, part, :])
-    load_pair()
-    wait("s", m_w1, out0, ("arr0", 56))
-    in0 = dma("s", W[row, 2048:4096], T.land0[:])
-    wait("s", ownM, ("arrM", 56))
-    inM = dma("s", T.mapw[row, 512:2048], T.landM[:, part, :])
+    staged.append(stage(1))
+    wait("s", arrS, *sS)
+    wait("a", arrS, *sS)
+    l_sd = dma("s", (T.sd32[:], XS[ins_, 96:120, :]))
+    l_st = dma("a", (T.st32[:], XS[ins_, 120:128, :]))
+    l_tb = dma("a", (T.tb32[:], XS[ins_, 64:96, :]))
+    l_nb = dma("s", (T.l32[:, 0:128], XS[ins_, 0:32, :]), (T.l32[:, 128:256], XS[ins_, 32:64, :]))
+    wait("gq", arrS)
+    for c in range(2, NCH):
+        staged.append(stage(c))
+    tables_in = [dma("s", (tab[mine, R + CUTS[LONG]:R + 8192], T.pair[mine, CUTS[LONG]:8192]))]
+    for c in range(1, NCH):
+        send_chunk(c)
+    for c in range(LONG, NCH):
+        wait("s", arrived[c])
+        tables_in.append(dma("s", *lay_out(c, others)))
+    wait("s", *tables_in)
+    count["again"] = 2 * all_engines
+    repeated = [dma("s", (tab[:, R + 8192 + CUTS[LONG]:R + 16384], tab[:, R + CUTS[LONG]:R + 8192])),
+                ("again", count["again"])]
+    tables_in += [("fin%d" % c, all_engines) for c in range(LONG)]
 
-    psV, psB, psE = [T.psV0, T.psV1], [T.psB0, T.psB1], [T.psE0, T.psE1]
-    rm, nf, sc = [T.rm0, T.rm1], [T.nf0, T.nf1], [T.s0, T.s1]
+    wait("v", c_const, l_sd)
+    v_rot = ts(T.rot[:], T.sd32[:, 0:96].indirect(T.rotL[:, 0:6]), -256.0, None, Op.add)
+    wait("v", l_st)
+    v_st = ts(T.stp[:, 96:128], T.st32[:], -1.0, 15.0, Op.mult, Op.add)
+    wait("v", l_tb)
+    v_tb = ts(T.tbb[:], T.tb32[:], -256.0, 16.0, Op.add, Op.mult)
+    wait("p", v_rot)
+    for d in range(8):
+        s = 16 * ((7 - d) % 8)
+        ins = P.matmul(T.psV0[:, 12 * d:12 * d + 12], T.R2[:, s:s + 128], T.rot[:, 12 * d:12 * d + 12], True, True)
+    p_sd = done("p", ins)
+    wait("p", v_st, c_Z)
+    for p in range(16):
+        s = 96 - 32 * (p % 4)
+        ins = P.matmul(T.psO0[:, 128 * (p // 4):128 * (p // 4) + 128], T.stp[:, s:s + 128], T.Z[:, p:2048:16],
+                       p % 4 == 0, p % 4 == 3)
+    p_st = done("p", ins)
+    turns = [(h, b, k) for h in range(2) for b in range(2) for k in range(4)]
+    wait("p", v_tb)
+    for i, (h, b, k) in enumerate(turns):
+        c = 64 * h + 16 * k + 8 * b
+        ins = P.matmul(T.psV1[:, 8 * i:8 * i + 8], ident, T.tbb[:, c:c + 8], True, True)
+    p_tb = done("p", ins)
+    wait("v", p_sd)
+    x = ts(T.sdr[:], T.psV0[:, 0:96], 256.0, None, Op.add)
+    wait("v", x)
+    v_sd = done("v", V.tensor_copy(T.sd16[:], T.sdr[:, 0:96].indirect(T.rotL[:, 6:12])))
+    wait("v", l_nb)
+    v_l = done("v", V.tensor_copy(T.l16[:], T.l32[:]))
+    wait("a", p_st)
+    a_rep = done("a", A.activation(T.repI[:, 0:512], T.psO0[:, 0:512], Act.Copy))
+    wait("a", p_tb)
+    a_tb = done("a", A.activation(T.tbw[:], T.psV1[:, 0:128], Act.Copy))
 
-    def open_round(t):
-        h = t & 1
-        wait("p", g_const, g_tb[h], l_own)
-        for r in range(16):
-            a = 1024 * h + 256 * (r % 4)
-            P.matmul(T.psO[:, 0:64], sel(T.selA, r), T.tbrow[:, a + r // 4:a + 256:4], r == 0, False)
+    def spread(src, a, bank, ranks):
+        for i, q in enumerate(ranks):
+            ins = P.transpose(bank[:, 128 * i:128 * i + 128], src[:, a + q:a + q + 128], ident)
+        return done("p", ins)
+
+    wait("p", a_rep)
+    first = [spread(T.repI, 128 * x, psT[x], range(8)) for x in range(4)]
+    wait("v", v_sd)
+    wait("a", v_sd)
+    for q in range(4):
+        a, b = 512 + G * q, 512 + G * (q + 4)
+        mv = ts(T.mapw[:, a:a + G], T.mapw[:, 0:512].indirect(T.sd16[:, 12 * q:12 * q + 12]), T.bq[:, q:q + 1], None, Op.add)
+        ma = done("a", A.activation(T.mapw[:, b:b + G], T.mapw[:, 0:512].indirect(T.sd16[:, 12 * q + 48:12 * q + 60]),
+                                    Act.Identity, bias=T.bq[:, q + 4:q + 5]))
+    numbers = T.mapw[:, 0:2048]
+
+    def compose_mm(h, bank, *marks):
+        wait("p", *marks)
+        for j in range(2):
+            for i, (_, b, k) in enumerate(turns[:8]):
+                a = 2048 * h + 1024 * j + 256 * k + 128 * b
+                ins = P.matmul(bank[:, 64 * j + 8 * i:64 * j + 8 * i + 8], T.crow[:, a:a + 128], T.selC[:], True, True)
+        return done("p", ins)
+
+    wait("v", mv, ma, v_l)
+    wait("a", mv, ma, v_l)
+    u0 = done("v", V.tensor_copy(T.crow[:, 0:1024], numbers.indirect(T.l16[:, 0:64])))
+    z0 = done("a", A.activation(T.crow[:, 1024:2048], numbers.indirect(T.l16[:, 128:192]), Act.Copy))
+    c0 = compose_mm(0, T.psO1, u0, z0)
+    for x in range(4):
+        wait("v", first[x])
+        w1 = done("v", V.tensor_copy(W[:, 1024 * x:1024 * x + 1024], psT[x][:]))
+    wait("v", c0)
+    lists = [done("v", V.tensor_copy(T.cmp16[:, 0:128], T.psO1[:, 0:128]))]
+    u1 = done("v", V.tensor_copy(T.crow[:, 2048:2304], numbers.indirect(T.l16[:, 64:80])))
+    done("a", A.activation(T.crow[:, 2304:3072], numbers.indirect(T.l16[:, 80:128]), Act.Copy))
+    z1 = done("a", A.activation(T.crow[:, 3072:4096], numbers.indirect(T.l16[:, 192:256]), Act.Copy))
+
+    def open_offsets(t):
         for b in range(2):
-            a = 256 * h + 128 * b
-            P.matmul(psV[b][:, 0:128], T.ownb[:, a:a + 128], T.idb[:], True, False)
+            a = 64 * (t & 1) + 32 * b
+            P.matmul(psO[b][:, 0:32], ident, T.tbw[:, a:a + 32], True, False)
 
-    repeated = []
+    def open_sums(t):
+        for b in range(2):
+            a = 256 * (t & 1) + 128 * b
+            P.matmul(psV[b][:, 0:128], tab[:, a:a + 128], ident, True, False)
 
-    def compose(h):
-        wait("v", inM)
-        wait("a", inM)
-        cv = done("v", V.tensor_copy(T.crow[:, 0:1024], T.mapw[:, 0:2048].indirect(T.l16[:, 64 * h:64 * h + 64])))
-        ca = done("a", A.activation(T.crow[:, 1024:2048],
-                                    T.mapw[:, 0:2048].indirect(T.l16[:, 128 + 64 * h:192 + 64 * h]), Act.Copy))
-        a, b, c = COPY_CUTS[2 - 2 * h:5 - 2 * h]
-        done("v", V.tensor_copy(T.pairb[:, 8192 + a:8192 + b], T.pairb[:, a:b]))
-        repeated.append(done("a", A.activation(T.pairb[:, 8192 + b:8192 + c], T.pairb[:, b:c], Act.Copy)))
-        wait("p", cv, ca)
-        for r in range(16):
-            ins = P.matmul(T.psC[:, 0:128], sel(T.selA, r), T.crow[:, r:2048:16], r == 0, r == 15)
-        wait("v", done("p", ins), c_base)
-        x = done("v", V.tensor_scalar(T.f1[:], T.psC[:, 0:128], 0.0, 1792.0, Op.is_ge, Op.mult))
-        wait("v", x)
-        x = done("v", V.tensor_tensor(T.f2[:], T.psC[:, 0:128], T.f1[:], Op.add))
-        wait("v", x)
-        for j in range(2):
-            a = 128 * j + 64 * h
-            x = done("v", V.tensor_tensor(T.f3[:, 64 * j:64 * j + 64], T.f2[:, 64 * j:64 * j + 64],
-                                          T.base[:, a:a + 64], Op.add))
-        wait("v", x)
-        for j in range(2):
-            a = 128 * j + 64 * h
-            x = done("v", V.tensor_copy(T.cmp16[:, a:a + 64], T.f3[:, 64 * j:64 * j + 64]))
-        return x
+    def low_rows(x, bank):
+        return done("p", P.transpose(bank[0:8, 128 * (x % 2):128 * (x % 2) + 128], rm[x][:, 16:129:16], T.idf[:]))
 
-    open_round(0)
-    lists = c_l
+    def state_rows(x, bank):
+        return done("p", P.transpose(bank[0:8, 128 * (x % 2):128 * (x % 2) + 128], sc[x][:, 15:128:16], ident))
+
+    c1 = compose_mm(1, T.psV0, u1, z1)
+    wait("p", a_tb, lists[0])
+    open_offsets(0)
+    window = [w1]
     for t in range(RD):
         h, last = t & 1, t == RD - 1
-        win, tile = (W[:, 0:2048], T.l16) if t == 0 else (W[:, 0:4096], T.cmp16)
+        tables, ready = (tab[:, R:R + 8192], tables_in) if t == 0 else (tab[:, R:R + WIDE], repeated)
+
+        def offsets(b, summed):
+            wait("v", summed)
+            c = slice(32 * b, 32 * b + 32)
+            if t > 0:
+                return ts(T.off[:, c], psO[b][:, 0:32], 12991.0, None, Op.add)
+            x = ts(T.o1[:, c], psO[b][:, 0:32], 12991.0, None, Op.add)
+            wait("v", x)
+            x = ts(T.o2[:, c], T.o1[:, c], 8191, None, Op.bitwise_and)
+            wait("v", x)
+            return done("v", V.tensor_copy(T.off[:, c], T.o2[:, c]))
+
+        def pairs(q, made, c0, c1):
+            wait(q, made, *ready)
+            out, src = T.xb[:, 128 * c0:128 * c1], tables.indirect(T.off[:, 8 * c0:8 * c1])
+            return done(q, V.tensor_copy(out, src) if q == "v" else A.activation(out, src, Act.Copy))
+
+        def add(mark, c0, c1):
+            wait("p", mark)
+            for c in range(c0, c1):
+                ins = P.matmul(psV[c // 4][:, 0:128], T.xb[:, 128 * c:128 * c + 128], ident, False, c % 4 == 3)
+            return ins
+
         for q in ("v", "a"):
-            wait(q, lists, window)
-            if t == 1:
-                wait(q, in0)
-        for k in range(4):
-            a, c = 64 * h + 16 * k, 256 * k
-            u = done("v", V.tensor_scalar(T.ub[:, c:c + 256], win.indirect(tile[:, a:a + 16]), -1.0, None, Op.mult))
-            z = done("a", A.activation(T.zb[:, c:c + 256], win.indirect(tile[:, 128 + a:144 + a]), Act.Copy))
-            wait("p", u)
-            for j in range(4):
-                P.matmul(T.psO[:, 0:64], sel(T.selA, 4 * j + k), T.ub[:, c + j:c + 256:4], False, False)
-            wait("p", z)
-            for j in range(4):
-                ins = P.matmul(T.psO[:, 0:64], sel(T.selB, 4 * j + k), T.zb[:, c + j:c + 256:4], False,
-                               k == 3 and j == 3)
-        wait("v", done("p", ins))
-        if t < 2:
-            x = done("v", V.tensor_scalar(T.o1[:], T.psO[:, 0:64], 12991.0, None, Op.add))
-            wait("v", x)
-            x = done("v", V.tensor_scalar(T.o2[:], T.o1[:], 8191, None, Op.bitwise_and))
-            wait("v", x)
-            x = done("v", V.tensor_copy(T.off[:], T.o2[:]))
-            tables = T.pairb[:, 0:8192]
-        else:
-            x = done("v", V.tensor_scalar(T.off[:], T.psO[:, 0:64], 12991.0, None, Op.add))
-            tables = T.pairb[:, 0:WIDE]
-        wait("v", x, *l_pair, *repeated)
-        wait("a", x, *l_pair, *repeated)
+            wait(q, lists[h], *window)
         summed = []
-        for b, (c0, c1, c2) in enumerate(((0, 16, 32), (32, 32 + NV, 64))):
-            xv = done("v", V.tensor_copy(T.xb[:, 16 * c0:16 * c1], tables.indirect(T.off[:, c0:c1])))
-            xa = done("a", A.activation(T.xb[:, 16 * c1:16 * c2], tables.indirect(T.off[:, c1:c2]), Act.Copy))
-            wait("p", xv, xa)
-            for k in range(4):
-                ins = P.matmul(psV[b][:, 0:128], T.xb[:, 512 * b + k:512 * b + 512:4], T.idb[:], False, k == 3)
-            summed.append(done("p", ins))
-        back, low = [], []
+        for i in range(4):
+            a, c = 128 * h + 16 * i, 256 * i
+            u = done("v", V.tensor_copy(T.ub[:, c:c + 256], W[:, 0:4096].indirect(T.cmp16[:, a:a + 16])))
+            z = done("a", A.activation(T.zb[:, c:c + 256], W[:, 0:4096].indirect(T.cmp16[:, 64 + a:80 + a]), Act.Copy))
+            for mark, buf, m in ((u, T.ub, T.selU), (z, T.zb, T.selZ)):
+                wait("p", mark)
+                for j in range(2):
+                    o = 16 * (i % 2) + 8 * j
+                    ins = P.matmul(psO[i // 2][:, o:o + 8], buf[:, c + 128 * j:c + 128 * j + 128], m[:], False,
+                                   i % 2 == 1 and j == 1 and buf is T.zb)
+            if i % 2 == 1:
+                summed.append(done("p", ins))
+            if i == 2:
+                off0 = offsets(0, summed[0])
+        if t == 0:
+            wait("v", c1)
+            lists.append(done("v", V.tensor_copy(T.cmp16[:, 128:256], T.psV0[:, 0:128])))
+            wait("p", lists[1], *tables_in)
+            open_sums(0)
+        x0 = pairs("v", off0, 0, 1)
+        x1 = pairs("a", off0, 1, 3)
+        x2 = pairs("a", off0, 3, 4)
+        off1 = offsets(1, summed[1])
+        x3 = pairs("v", off1, 4, 6)
+        x4 = pairs("a", off1, 6, 8)
+        add(x0, 0, 1)
+        add(x1, 1, 3)
+        summed = [done("p", add(x2, 3, 4))]
+        add(x3, 4, 6)
+        summed.append(done("p", add(x4, 6, 8)))
+        if last:
+            state_rows(0, psT[0])
+            state_rows(1, psT[0])
+            low_rows(0, psO[0])
+            half0 = low_rows(1, psO[0])
+            wait("a", half0)
+            done("a", A.activation(T.res[0:8, 0:256], psT[0][0:8, 0:256], Act.Identity, bias=15.0, scale=-1.0))
+            done("a", A.activation(T.res[0:8, 512:768], psO[0][0:8, 0:256], Act.Copy))
+        found = []
         for b in range(2):
-            wait("v", summed[b], g_const)
-            s1 = done("v", V.tensor_tensor_scan(rm[b][:, 1:129], T.c0[:], psV[b][:, 0:128], 0.0, Op.add, Op.min))
+            x = 2 * h + b
+            wait("v", summed[b], g_c2)
+            s1 = done("v", V.tensor_tensor_scan(rm[x][:, 1:129], T.c0[:], psV[b][:, 0:128], 0.0, Op.add, Op.min))
             wait("v", s1)
-            x = done("v", V.tensor_tensor(nf[b][:], psV[b][:, 0:128], rm[b][:, 0:128], Op.is_ge))
-            wait("v", x)
-            s2 = done("v", V.tensor_tensor_scan(sc[b][:], nf[b][:], T.c2[:], 0.0, Op.mult, Op.max))
+            ge = done("v", V.tensor_tensor(nf[b][:], psV[b][:, 0:128], rm[x][:, 0:128], Op.is_ge))
+            wait("v", ge)
+            found.append(done("v", V.tensor_tensor_scan(sc[x][:], nf[b][:], T.c2[:], 0.0, Op.mult, Op.max)))
             if last:
                 wait("p", s1)
-                low.append(done("p", P.transpose(psE[b][0:8, 0:128], rm[b][:, 16:129:16], T.idf[:])))
-            wait("p", s2)
-            back.append(done("p", P.matmul(psB[b][0:8, 0:128], sc[b][:, 15:128:16], T.idb[:], True, True)))
+                lows = low_rows(x, psO[1])
+                wait("p", found[b])
+                states = state_rows(x, psT[1])
         if not last:
-            c = 256 * t
-            wait("a", back[0])
-            r0 = done("a", A.activation(T.rows[0:8, c:c + 128], T.psB0[0:8, 0:128], Act.Copy))
-            wait("v", back[1])
-            r1 = done("v", V.tensor_copy(T.rows[0:8, c + 128:c + 256], T.psB1[0:8, 0:128]))
-            land = T["land%d" % (t + 1)]
-            wait("s", r0, r1)
-            out = dma("s", land[rank:64:8], T.rows[0:8, c:c + 256])
-            wait("gq", out)
-            send_states(t + 1)
-            wait("s", out, ("arr%d" % (t + 1), 56))
-            window = dma("s", W[row, 2048 * h:2048 * h + 2048], land[:])
-            if t == RD - 2:
-                for b in range(2):
-                    low.append(done("p", P.transpose(psE[b][0:8, 0:128], rm[b][:, 16:129:16], T.idf[:])))
-                    wait("a", low[b])
-                    x = done("a", A.activation(T.erow[0:8, 128 * b:128 * b + 128], psE[b][0:8, 0:128], Act.Copy))
+            a, turned = 2048 * h, []
+            for b in range(2):
+                wait("a", found[b])
+                x = done("a", A.activation(rep[b][:, 0:128], sc[2 * h + b][:, 0:128].indirect(T.repL[:]), Act.Copy))
                 wait("p", x)
-                wait("v", r0, r1)
-                done("v", V.tensor_scalar(T.yrow[0:8, 0:256], T.rows[0:8, c:c + 256], -1.0, 15.0, Op.mult, Op.add))
-            open_round(t + 1)
-            if t < 2:
-                lists = compose(1 - t)
+                turned += [spread(rep[b], 0, psT[2 * b + j], range(4 * j, 4 * j + 4)) for j in range(2)]
+            window = []
+            for j, q in enumerate("vavv"):
+                wait(q, turned[j])
+                out, src = W[:, a + 512 * j:a + 512 * j + 512], psT[j][:, 0:512]
+                window.append(done(q, V.tensor_copy(out, src) if q == "v" else A.activation(out, src, Act.Copy)))
+            open_offsets(t + 1)
+            open_sums(t + 1)
         else:
-            wait("a", low[0])
-            done("a", A.activation(T.erow[0:8, 256:384], T.psE0[0:8, 0:128], Act.Copy))
-            wait("a", back[0])
-            y0 = done("a", A.activation(T.yrow[0:8, 256:384], T.psB0[0:8, 0:128], Act.Identity, bias=15.0, scale=-1.0))
-            wait("a", low[1])
-            e1 = done("a", A.activation(T.erow[0:8, 384:512], T.psE1[0:8, 0:128], Act.Copy))
-            wait("v", back[1])
-            y1 = done("v", V.tensor_scalar(T.yrow[0:8, 384:512], T.psB1[0:8, 0:128], -1.0, 15.0, Op.mult, Op.add))
-            wait("a", e1)
-            wait("a", dma("a", T.e[:], T.erow[0:8, :]))
-            wait("s", y0, y1)
-            wait("s", dma("s", T.y[:], T.yrow[0:8, :]))
-
-    for sem, val in count.items():
-        if max([v for (q, s), v in seen.items() if s == sem] + [0]) < val:
-            wait("gq", (sem, val))
+            wait("a", lows)
+            e1 = done("a", A.activation(T.res[0:8, 768:1024], psO[1][0:8, 0:256], Act.Copy))
+            wait("v", states)
+            y1 = ts(T.res[0:8, 256:512], psT[1][0:8, 0:256], -1.0, 15.0, Op.mult, Op.add)
+            wait("s", e1, y1)
+            out = dma("s", (T.XO[outs], T.res[0:8, :]))
+            wait("gq", out)
+            arrO = send(lambda r: T.XO[8 * r + rank], lambda r: T.XO[8 * r + rank], "arrO", 0, 2)
+            wait("s", out, arrO)
+            wait("a", out, arrO)
+            wait("a", dma("a", (T.e[:], T.XO[ins_, 64:128, :])))
+            wait("s", dma("s", (T.y[:], T.XO[ins_, 0:64, :])))
+    finish()

from concourse.bass import DstId, RemoteDMATransfer
from concourse.mybir import AluOpType as Op, ActivationFunctionType as Act

N, R, G, RD = 8, 512, 192, 6
CUTS = [0, 1536, 3584, 5632, 7168, 8192]
NCH = len(CUTS) - 1
LONG = 3
WIDE = 17088

BF, F32, I32, U16 = "bfloat16", "float32", "int32", "uint16"
SCRATCH = {
    "XS": ("dram", [64, 128, 64], I32),
    "XO": ("dram", [64, 128, 8], F32),
    "l32": ("sbuf", [128, 256], I32), "l16": ("sbuf", [128, 256], U16), "cmp16": ("sbuf", [128, 256], U16),
    "tb32": ("sbuf", [128, 128], I32), "tbb": ("sbuf", [128, 128], BF), "tbw": ("sbuf", [128, 128], BF),
    "sd32": ("sbuf", [128, 96], I32), "rot": ("sbuf", [128, 96], BF), "sdr": ("sbuf", [128, 96], F32),
    "sd16": ("sbuf", [128, 96], U16), "st32": ("sbuf", [128, 32], I32), "stp": ("sbuf", [128, 224], BF),
    "tab": ("sbuf", [128, R + WIDE], BF),
    "W": ("sbuf", [128, 4096], BF), "mapw": ("sbuf", [128, 2048], BF), "crow": ("sbuf", [128, 4096], BF),
    "ub": ("sbuf", [128, 1024], BF), "zb": ("sbuf", [128, 1024], BF), "xb": ("sbuf", [128, 1024], BF),
    "nI": ("sbuf", [128, 256], BF), "p8": ("sbuf", [128, 8], I32), "e8": ("sbuf", [128, 8], I32),
    "iv": ("sbuf", [128, 8], I32), "fv": ("sbuf", [128, 8], F32), "col": ("sbuf", [128, 16], F32),
    "bq": ("sbuf", [128, 8], F32), "bx": ("sbuf", [128, 8], F32),
    "t1": ("sbuf", [128, 16], F32), "t2": ("sbuf", [128, 16], F32), "t3": ("sbuf", [128, 16], F32),
    "rotL": ("sbuf", [128, 16], U16), "repL": ("sbuf", [128, 8], U16),
    "Z": ("sbuf", [128, 2048], BF), "R2": ("sbuf", [128, 256], BF), "idf": ("sbuf", [128, 128], F32),
    "selU": ("sbuf", [128, 8], BF), "selZ": ("sbuf", [128, 8], BF), "selC": ("sbuf", [128, 8], BF),
    "c0": ("sbuf", [128, 128], F32), "c2": ("sbuf", [128, 128], BF),
    "o1": ("sbuf", [128, 64], I32), "o2": ("sbuf", [128, 64], I32), "off": ("sbuf", [128, 64], U16),
    "nf0": ("sbuf", [128, 128], BF), "nf1": ("sbuf", [128, 128], BF),
    "rep0": ("sbuf", [128, 144], BF), "rep1": ("sbuf", [128, 144], BF), "repI": ("sbuf", [128, 528], BF),
    "res": ("sbuf", [128, 1024], F32),
}
for _x in range(4):
    SCRATCH["rm%d" % _x] = ("sbuf", [128, 136], F32)
    SCRATCH["s%d" % _x] = ("sbuf", [128, 128], BF)
    SCRATCH["psT%d" % _x] = ("psum", [128, 1024], BF)
for _c in range(NCH):
    _w = CUTS[_c + 1] - CUTS[_c] + (R if _c == 0 else 0)
    SCRATCH["stage%d" % _c] = ("dram", [8, 128, _w // 8], BF)
    SCRATCH["land%d" % _c] = ("dram", [8, 128, _w // 8], BF)
for _n in ("psO0", "psO1", "psV0", "psV1"):
    SCRATCH[_n] = ("psum", [128, 512], F32)

SEMAPHORES = (["v", "a", "p", "gq", "left", "iss", "arrS", "arrO", "again"] + ["arr%d" % c for c in range(NCH)]
              + ["rel%d" % c for c in range(LONG)] + ["fin%d" % c for c in range(LONG)]
              + ["d%d" % i for i in range(60)])


def rank_program(g, core, T, topo):
    rank = T.rank_of(core)

    def helpers(r):
        me = T.cores[r]
        near = [k for k in topo.cores_of(me) if topo.die(k) == topo.die(me) and k not in T.cores]
        free = [k for k in near if all(topo.may_write(k, c) for c in T.cores)][0]
        rest = [k for k in near if k != free]
        return {"any": free, "plane": rest[0], "gather": rest[1]}

    role = [(r, name) for r in range(N) for name, k in helpers(r).items() if k == core]
    if rank is None and not role:
        return
    queue = {"s": g.sync, "gq": g}
    if rank is not None:
        V, A, P = g.vector, g.scalar, g.tensor
        queue.update({"v": V, "a": A, "p": P})
    count, seen, ndma = {}, {}, [0]
    tab = T.tab

    def wait(q, *marks):
        for sem, val in marks:
            if seen.get((q, sem), 0) < val:
                queue[q].wait_ge(T.sem[sem], val)
                seen[(q, sem)] = val

    def done(q, ins):
        count[q] = count.get(q, 0) + 1
        ins.then_inc(T.sem[q], 1)
        return (q, count[q])

    def dma(q, *copies):
        sem = "d%d" % ndma[0]
        ndma[0] += 1
        for out, in_ in copies:
            queue[q].dma_start(out, in_).then_inc(T.sem[sem], 16)
        count[sem] = 16 * len(copies)
        return (sem, count[sem])

    def engine_plan(src, turn, near):
        me = T.cores[src]
        order = [(src + 1 + i) % N for i in range(N - 1)]
        far = [r for r in order if topo.chip(T.cores[r]) != topo.chip(me)]
        lanes = sorted(set.intersection(*[set(topo.engines(me, T.cores[r])) for r in far]))
        one, two = lanes[turn % 2::2], lanes[1 - turn % 2::2]
        sets = [[e] for e in one] + [two[0:2], two[2:4]]
        plan = {far[(i + 2 * turn) % len(far)]: sets[i] for i in range(len(far))}
        for r in order:
            if r not in plan:
                plan[r] = [e for e in topo.engines(me, T.cores[r]) if e not in lanes][:near]
        return plan

    def send(src_of, dst_of, sem, turn, near):
        fused([(src_of(r), T.cores[r], dst_of(r), sem, engines) for r, engines in engine_plan(rank, turn, near).items()])
        count[sem] = sum(len(engine_plan(q, turn, near)[rank]) for q in range(N) if q != rank)
        return (sem, count[sem])

    def fused(writes):
        tr = []
        for src, to, dst, sem, engines in writes:
            rid, pid, _ = topo.addr(to)
            tr.append(RemoteDMATransfer(dst_ids=[DstId(rid=rid, pnc=pid)], dma_engine_mask=sum(1 << e for e in engines),
                                        remote_sem=T.sem[sem], srcs=[src], dsts=[dst]))
        g.remote_dma_fused(tr, local_sem=T.sem.left)
        count["left"] = count.get("left", 0) + sum(len(w[4]) for w in writes)

    def long_plan(src):
        me, hs = T.cores[src], helpers(src)
        order = [(src + 1 + i) % N for i in range(N - 1)]
        far = [r for r in order if topo.chip(T.cores[r]) != topo.chip(me)]
        plane = [r for r in far if topo.may_write(hs["plane"], T.cores[r])]
        cross = [r for r in far if r not in plane]
        lanes = topo.engines(me, T.cores[far[0]])
        spare = [e for e in topo.engines(me, hs["any"]) if e not in lanes]
        ways = ([(r, None) for r in cross[:2]] + [(r, hs["any"]) for r in cross[2:]]
                + [(r, None) for r in order if r not in far] + [(src, None)] + [(r, hs["plane"]) for r in plane])
        sets = [lanes[0:4:2], lanes[4:8:2], lanes[1:4:2], lanes[5:8:2], spare[0:4:2], spare[1:4:2], spare[4:6], spare[6:8]]
        return {r: (via, engines) for (r, via), engines in zip(ways, sets)}

    def cut(c):
        buf = T["land%d" % c]
        return CUTS[c], CUTS[c + 1], 16 * (CUTS[c + 1] - CUTS[c]) // buf.shape[2]

    def lay_out(c, runs):
        a, b, rows = cut(c)
        buf = T["land%d" % c]
        return ([(tab[16 * x:16 * y, R + a:R + b], buf[x:y, 0:rows, :]) for x, y in runs]
                + [(tab[16 * x:16 * y, 0:R], buf[x:y, rows:128, :]) for x, y in runs if c == 0])

    def finish():
        for sem, val in count.items():
            if max([v for (q, s), v in seen.items() if s == sem] + [0]) < val:
                wait("gq", (sem, val))

    if rank is None:
        owner, name = role[0]
        to = T.cores[owner]
        for c in range(LONG):
            if name == "gather":
                wait("s", ("arr%d" % c, sum(2 if long_plan(q)[owner][0] is None else 4 for q in range(N))))
                wait("gq", dma("s", *lay_out(c, [(0, N)])))
                cols = slice(0 if c == 0 else R + CUTS[c], R + CUTS[c + 1])
                fused([(tab[:, cols], to, tab[:, cols], "fin%d" % c, topo.engines(core, to))])
            else:
                mine = [r for r, (via, engines) in long_plan(owner).items() if via == core]
                wait("gq", ("rel%d" % c, 2 * len(mine)))
                lanes = topo.engines(core, T.cores[mine[0]])
                fused([(T["stage%d" % c][r], helpers(r)["gather"], T["land%d" % c][owner], "arr%d" % c,
                        lanes[4 * i:4 * i + 4]) for i, r in enumerate(mine)])
        if name == "gather":
            for a, n in ((8192, CUTS[LONG]), (16384, WIDE - 16384)):
                fused([(tab[:, R:R + n], to, tab[:, R + a:R + a + n], "again", topo.engines(core, to))])
        finish()
        return

    W, XS, col, nI = T.W, T.XS, T.col, T.nI
    ident = T.Z[:, 0:128]
    others = [(a, b) for a, b in ((0, rank), (rank + 1, N)) if a < b]
    mine = slice(16 * rank, 16 * rank + 16)
    outs, ins_ = slice(rank, 64, 8), slice(8 * rank, 8 * rank + 8)
    all_engines = len(topo.engines(helpers(rank)["gather"], core))
    psO, psV, psT = [T.psO0, T.psO1], [T.psV0, T.psV1], [T["psT%d" % x] for x in range(4)]
    rm, sc = [T["rm%d" % x] for x in range(4)], [T["s%d" % x] for x in range(4)]
    nf, rep = [T.nf0, T.nf1], [T.rep0, T.rep1]

    def stage(c):
        a, b, rows = cut(c)
        buf, runs = T["stage%d" % c], [(0, N)] if c < LONG else others
        return dma("s", *([(buf[x:y, 0:rows, :], T.pair[16 * x:16 * y, a:b]) for x, y in runs]
                          + [(buf[x:y, rows:128, :], T.own[16 * x:16 * y, :]) for x, y in runs if c == 0]))

    sS = [dma("s", (XS[outs, 0:32, :], T.nb[:]), (XS[outs, 32:64, :], T.th[:]), (XS[outs, 64:96, :], T.tb[:])),
          dma("a", (XS[outs, 96:120, :], T.sd[:]), (XS[outs, 120:128, :], T.st[:]))]
    staged = [stage(0)]

    g_p = done("gq", g.iota(T.p8[:], [[0, 8]], 0, 1))
    g_n = done("gq", g.iota(nI[:], [[0, 2], [1, 128]], 0, 0, allow_small_or_imprecise_dtypes=True))
    g_c2 = done("gq", g.iota(T.c2[:], [[0, 8], [-1, 16]], 15, 0, allow_small_or_imprecise_dtypes=True))

    def ts(out, in0, s1, s2, op0, op1=None):
        if op1 is None:
            return done("v", V.tensor_scalar(out, in0, s1, None, op0))
        return done("v", V.tensor_scalar(out, in0, s1, s2, op0, op1))

    x = done("v", V.memset(T.c0[:], 0.0))
    for buf in [T.stp[:], T.rep0[:, 128:144], T.rep1[:, 128:144], T.repI[:, 512:528]] + [m[:, 0:8] for m in rm]:
        done("v", V.memset(buf, 0.0))
    wait("v", x, g_p)
    done("v", V.memset(T.c0[:, 0:128:16], 1e29))
    p1 = T.p8[:, 0:1]
    ts(T.iv[:, 0:1], p1, 127, None, Op.bitwise_and)
    ts(T.iv[:, 1:2], p1, 4, None, Op.arith_shift_right)
    ts(T.iv[:, 2:3], p1, 15, None, Op.bitwise_and)
    x = ts(T.e8[:], T.p8[:], 7, None, Op.bitwise_and)
    wait("v", x)
    x = done("v", V.tensor_copy(T.fv[:, 0:3], T.iv[:, 0:3]))
    ts(T.repL[:], T.e8[:], 16.0, 15.0, Op.mult, Op.add)
    wait("v", x, g_n)
    pf, gf, lf = [T.fv[:, i:i + 1] for i in range(3)]
    cM0, cM1, cU, cZ, cH, cR, cD, cE, cC = [col[:, i:i + 1] for i in range(9)]
    c_z = ts(T.Z[:, 0:256], nI[:], pf, None, Op.is_equal)
    ts(cD, gf, -12.0, lf, Op.mult, Op.add)
    ts(cE, gf, 12.0, lf, Op.mult, Op.add)
    ts(cR, gf, -16.0, lf, Op.mult, Op.add)
    ts(cM0, lf, 0.0, None, Op.is_equal)
    ts(cM1, lf, 1.0, None, Op.is_equal)
    ts(cU, lf, 0.0, -1.0, Op.is_equal, Op.mult)
    ts(cZ, lf, 0.0, -592.0, Op.is_equal, Op.mult)
    ts(cH, lf, 1.0, 128.0, Op.is_equal, Op.mult)
    x = ts(T.t3[:, 12:16], nI[:, 0:4], 8.0, gf, Op.mult, Op.add)
    wait("v", x)
    ts(T.t1[:, 0:6], nI[:, 0:6], 16.0, cD, Op.mult, Op.add)
    ts(T.t1[:, 6:12], nI[:, 0:6], 16.0, cE, Op.mult, Op.add)
    ts(cC, cM0, cH, None, Op.add)
    ts(T.bq[:], nI[:, 0:8], gf, cM1, Op.subtract, Op.mult)
    x = ts(T.bx[:, 0:4], T.t3[:, 12:16], cM1, None, Op.mult)
    ts(T.R2[:], nI[:], -112.0, cR, Op.add, Op.is_equal)
    wait("v", x)
    ts(T.t2[:, 0:6], T.t1[:, 0:6], 0.0, 96.0, Op.is_lt, Op.mult)
    x = ts(T.t2[:, 6:12], T.t1[:, 6:12], 96.0, -96.0, Op.is_ge, Op.mult)
    for m, w in ((T.selC, cC), (T.selU, cU), (T.selZ, cZ)):
        ts(m[:], nI[:, 0:8], gf, w, Op.is_equal, Op.mult)
    wait("v", x)
    x = done("v", V.tensor_tensor(T.t3[:, 0:12], T.t1[:, 0:12], T.t2[:, 0:12], Op.add))
    for a in range(4):
        ts(T.mapw[:, 128 * a:128 * a + 128], nI[:, 0:128], cM0, T.bx[:, a:a + 1], Op.mult, Op.add)
    wait("v", x)
    c_const = done("v", V.tensor_copy(T.rotL[:, 0:12], T.t3[:, 0:12]))
    x = c_z
    for n in (256, 512, 1024):
        wait("a", x)
        x = done("a", A.activation(T.Z[:, n:2 * n], T.Z[:, 0:n], Act.Copy))
    c_Z = x
    done("a", A.activation(T.idf[:], ident, Act.Copy))

    arrived = {}

    def send_chunk(c):
        wait("gq", staged[c])
        st_, la = T["stage%d" % c], T["land%d" % c]
        if c >= LONG:
            arrived[c] = send(lambda r: st_[r], lambda r: la[rank], "arr%d" % c, c + 1, 8)
            return
        fused([(st_[r], via, st_[r], "rel%d" % c, engines) if via is not None
               else (st_[r], helpers(r)["gather"], la[rank], "arr%d" % c, engines)
               for r, (via, engines) in long_plan(rank).items()])
        count["fin%d" % c] = all_engines

    wait("gq", *sS)
    arrS = send(lambda r: XS[8 * r + rank], lambda r: XS[8 * r + rank], "arrS", 0, 2)
    g.sem_inc(T.sem.iss, 1)
    count["iss"] = 1
    send_chunk(0)
    wait("s", ("iss", 1))
    staged.append(stage(1))
    wait("s", arrS, *sS)
    wait("a", arrS, *sS)
    l_sd = dma("s", (T.sd32[:], XS[ins_, 96:120, :]))
    l_st = dma("a", (T.st32[:], XS[ins_, 120:128, :]))
    l_tb = dma("a", (T.tb32[:], XS[ins_, 64:96, :]))
    l_nb = dma("s", (T.l32[:, 0:128], XS[ins_, 0:32, :]), (T.l32[:, 128:256], XS[ins_, 32:64, :]))
    wait("gq", arrS)
    for c in range(2, NCH):
        staged.append(stage(c))
    tables_in = [dma("s", (tab[mine, R + CUTS[LONG]:R + 8192], T.pair[mine, CUTS[LONG]:8192]))]
    for c in range(1, NCH):
        send_chunk(c)
    for c in range(LONG, NCH):
        wait("s", arrived[c])
        tables_in.append(dma("s", *lay_out(c, others)))
    wait("s", *tables_in)
    count["again"] = 2 * all_engines
    repeated = [dma("s", (tab[:, R + 8192 + CUTS[LONG]:R + 16384], tab[:, R + CUTS[LONG]:R + 8192])),
                ("again", count["again"])]
    tables_in += [("fin%d" % c, all_engines) for c in range(LONG)]

    wait("v", c_const, l_sd)
    v_rot = ts(T.rot[:], T.sd32[:, 0:96].indirect(T.rotL[:, 0:6]), -256.0, None, Op.add)
    wait("v", l_st)
    v_st = ts(T.stp[:, 96:128], T.st32[:], -1.0, 15.0, Op.mult, Op.add)
    wait("v", l_tb)
    v_tb = ts(T.tbb[:], T.tb32[:], -256.0, 16.0, Op.add, Op.mult)
    wait("p", v_rot)
    for d in range(8):
        s = 16 * ((7 - d) % 8)
        ins = P.matmul(T.psV0[:, 12 * d:12 * d + 12], T.R2[:, s:s + 128], T.rot[:, 12 * d:12 * d + 12], True, True)
    p_sd = done("p", ins)
    wait("p", v_st, c_Z)
    for p in range(16):
        s = 96 - 32 * (p % 4)
        ins = P.matmul(T.psO0[:, 128 * (p // 4):128 * (p // 4) + 128], T.stp[:, s:s + 128], T.Z[:, p:2048:16],
                       p % 4 == 0, p % 4 == 3)
    p_st = done("p", ins)
    turns = [(h, b, k) for h in range(2) for b in range(2) for k in range(4)]
    wait("p", v_tb)
    for i, (h, b, k) in enumerate(turns):
        c = 64 * h + 16 * k + 8 * b
        ins = P.matmul(T.psV1[:, 8 * i:8 * i + 8], ident, T.tbb[:, c:c + 8], True, True)
    p_tb = done("p", ins)
    wait("v", p_sd)
    x = ts(T.sdr[:], T.psV0[:, 0:96], 256.0, None, Op.add)
    wait("v", x)
    v_sd = done("v", V.tensor_copy(T.sd16[:], T.sdr[:, 0:96].indirect(T.rotL[:, 6:12])))
    wait("v", l_nb)
    v_l = done("v", V.tensor_copy(T.l16[:], T.l32[:]))
    wait("a", p_st)
    a_rep = done("a", A.activation(T.repI[:, 0:512], T.psO0[:, 0:512], Act.Copy))
    wait("a", p_tb)
    a_tb = done("a", A.activation(T.tbw[:], T.psV1[:, 0:128], Act.Copy))

    def spread(src, a, bank, ranks):
        for i, q in enumerate(ranks):
            ins = P.transpose(bank[:, 128 * i:128 * i + 128], src[:, a + q:a + q + 128], ident)
        return done("p", ins)

    wait("p", a_rep)
    first = [spread(T.repI, 128 * x, psT[x], range(8)) for x in range(4)]
    wait("v", v_sd)
    wait("a", v_sd)
    for q in range(4):
        a, b = 512 + G * q, 512 + G * (q + 4)
        mv = ts(T.mapw[:, a:a + G], T.mapw[:, 0:512].indirect(T.sd16[:, 12 * q:12 * q + 12]), T.bq[:, q:q + 1], None, Op.add)
        ma = done("a", A.activation(T.mapw[:, b:b + G], T.mapw[:, 0:512].indirect(T.sd16[:, 12 * q + 48:12 * q + 60]),
                                    Act.Identity, bias=T.bq[:, q + 4:q + 5]))
    numbers = T.mapw[:, 0:2048]

    def compose_mm(h, bank, *marks):
        wait("p", *marks)
        for j in range(2):
            for i, (_, b, k) in enumerate(turns[:8]):
                a = 2048 * h + 1024 * j + 256 * k + 128 * b
                ins = P.matmul(bank[:, 64 * j + 8 * i:64 * j + 8 * i + 8], T.crow[:, a:a + 128], T.selC[:], True, True)
        return done("p", ins)

    wait("v", mv, ma, v_l)
    wait("a", mv, ma, v_l)
    u0 = done("v", V.tensor_copy(T.crow[:, 0:1024], numbers.indirect(T.l16[:, 0:64])))
    z0 = done("a", A.activation(T.crow[:, 1024:2048], numbers.indirect(T.l16[:, 128:192]), Act.Copy))
    c0 = compose_mm(0, T.psO1, u0, z0)
    for x in range(4):
        wait("v", first[x])
        w1 = done("v", V.tensor_copy(W[:, 1024 * x:1024 * x + 1024], psT[x][:]))
    wait("v", c0)
    lists = [done("v", V.tensor_copy(T.cmp16[:, 0:128], T.psO1[:, 0:128]))]
    u1 = done("v", V.tensor_copy(T.crow[:, 2048:2304], numbers.indirect(T.l16[:, 64:80])))
    done("a", A.activation(T.crow[:, 2304:3072], numbers.indirect(T.l16[:, 80:128]), Act.Copy))
    z1 = done("a", A.activation(T.crow[:, 3072:4096], numbers.indirect(T.l16[:, 192:256]), Act.Copy))

    def open_offsets(t):
        for b in range(2):
            a = 64 * (t & 1) + 32 * b
            P.matmul(psO[b][:, 0:32], ident, T.tbw[:, a:a + 32], True, False)

    def open_sums(t):
        for b in range(2):
            a = 256 * (t & 1) + 128 * b
            P.matmul(psV[b][:, 0:128], tab[:, a:a + 128], ident, True, False)

    def low_rows(x, bank):
        return done("p", P.transpose(bank[0:8, 128 * (x % 2):128 * (x % 2) + 128], rm[x][:, 16:129:16], T.idf[:]))

    def state_rows(x, bank):
        return done("p", P.transpose(bank[0:8, 128 * (x % 2):128 * (x % 2) + 128], sc[x][:, 15:128:16], ident))

    c1 = compose_mm(1, T.psV0, u1, z1)
    wait("p", a_tb, lists[0])
    open_offsets(0)
    window = [w1]
    for t in range(RD):
        h, last = t & 1, t == RD - 1
        tables, ready = (tab[:, R:R + 8192], tables_in) if t == 0 else (tab[:, R:R + WIDE], repeated)

        def offsets(b, summed):
            wait("v", summed)
            c = slice(32 * b, 32 * b + 32)
            if t > 0:
                return ts(T.off[:, c], psO[b][:, 0:32], 12991.0, None, Op.add)
            x = ts(T.o1[:, c], psO[b][:, 0:32], 12991.0, None, Op.add)
            wait("v", x)
            x = ts(T.o2[:, c], T.o1[:, c], 8191, None, Op.bitwise_and)
            wait("v", x)
            return done("v", V.tensor_copy(T.off[:, c], T.o2[:, c]))

        def pairs(q, made, c0, c1):
            wait(q, made, *ready)
            out, src = T.xb[:, 128 * c0:128 * c1], tables.indirect(T.off[:, 8 * c0:8 * c1])
            return done(q, V.tensor_copy(out, src) if q == "v" else A.activation(out, src, Act.Copy))

        def add(mark, c0, c1):
            wait("p", mark)
            for c in range(c0, c1):
                ins = P.matmul(psV[c // 4][:, 0:128], T.xb[:, 128 * c:128 * c + 128], ident, False, c % 4 == 3)
            return ins

        for q in ("v", "a"):
            wait(q, lists[h], *window)
        summed = []
        for i in range(4):
            a, c = 128 * h + 16 * i, 256 * i
            u = done("v", V.tensor_copy(T.ub[:, c:c + 256], W[:, 0:4096].indirect(T.cmp16[:, a:a + 16])))
            z = done("a", A.activation(T.zb[:, c:c + 256], W[:, 0:4096].indirect(T.cmp16[:, 64 + a:80 + a]), Act.Copy))
            for mark, buf, m in ((u, T.ub, T.selU), (z, T.zb, T.selZ)):
                wait("p", mark)
                for j in range(2):
                    o = 16 * (i % 2) + 8 * j
                    ins = P.matmul(psO[i // 2][:, o:o + 8], buf[:, c + 128 * j:c + 128 * j + 128], m[:], False,
                                   i % 2 == 1 and j == 1 and buf is T.zb)
            if i % 2 == 1:
                summed.append(done("p", ins))
            if i == 2:
                off0 = offsets(0, summed[0])
        if t == 0:
            wait("v", c1)
            lists.append(done("v", V.tensor_copy(T.cmp16[:, 128:256], T.psV0[:, 0:128])))
            wait("p", lists[1], *tables_in)
            open_sums(0)
        x0 = pairs("v", off0, 0, 1)
        x1 = pairs("a", off0, 1, 3)
        x2 = pairs("a", off0, 3, 4)
        off1 = offsets(1, summed[1])
        x3 = pairs("v", off1, 4, 6)
        x4 = pairs("a", off1, 6, 8)
        add(x0, 0, 1)
        add(x1, 1, 3)
        summed = [done("p", add(x2, 3, 4))]
        add(x3, 4, 6)
        summed.append(done("p", add(x4, 6, 8)))
        if last:
            state_rows(0, psT[0])
            state_rows(1, psT[0])
            low_rows(0, psO[0])
            half0 = low_rows(1, psO[0])
            wait("a", half0)
            done("a", A.activation(T.res[0:8, 0:256], psT[0][0:8, 0:256], Act.Identity, bias=15.0, scale=-1.0))
            done("a", A.activation(T.res[0:8, 512:768], psO[0][0:8, 0:256], Act.Copy))
        found = []
        for b in range(2):
            x = 2 * h + b
            wait("v", summed[b], g_c2)
            s1 = done("v", V.tensor_tensor_scan(rm[x][:, 1:129], T.c0[:], psV[b][:, 0:128], 0.0, Op.add, Op.min))
            wait("v", s1)
            ge = done("v", V.tensor_tensor(nf[b][:], psV[b][:, 0:128], rm[x][:, 0:128], Op.is_ge))
            wait("v", ge)
            found.append(done("v", V.tensor_tensor_scan(sc[x][:], nf[b][:], T.c2[:], 0.0, Op.mult, Op.max)))
            if last:
                wait("p", s1)
                lows = low_rows(x, psO[1])
                wait("p", found[b])
                states = state_rows(x, psT[1])
        if not last:
            a, turned = 2048 * h, []
            for b in range(2):
                wait("a", found[b])
                x = done("a", A.activation(rep[b][:, 0:128], sc[2 * h + b][:, 0:128].indirect(T.repL[:]), Act.Copy))
                wait("p", x)
                turned += [spread(rep[b], 0, psT[2 * b + j], range(4 * j, 4 * j + 4)) for j in range(2)]
            window = []
            for j, q in enumerate("vavv"):
                wait(q, turned[j])
                out, src = W[:, a + 512 * j:a + 512 * j + 512], psT[j][:, 0:512]
                window.append(done(q, V.tensor_copy(out, src) if q == "v" else A.activation(out, src, Act.Copy)))
            open_offsets(t + 1)
            open_sums(t + 1)
        else:
            wait("a", lows)
            e1 = done("a", A.activation(T.res[0:8, 768:1024], psO[1][0:8, 0:256], Act.Copy))
            wait("v", states)
            y1 = ts(T.res[0:8, 256:512], psT[1][0:8, 0:256], -1.0, 15.0, Op.mult, Op.add)
            wait("s", e1, y1)
            out = dma("s", (T.XO[outs], T.res[0:8, :]))
            wait("gq", out)
            arrO = send(lambda r: T.XO[8 * r + rank], lambda r: T.XO[8 * r + rank], "arrO", 0, 2)
            wait("s", out, arrO)
            wait("a", out, arrO)
            wait("a", dma("a", (T.e[:], T.XO[ins_, 64:128, :])))
            wait("s", dma("s", (T.y[:], T.XO[ins_, 0:64, :])))
    finish()
